import numpy as np, ml_dtypes
CORES = [16,18,20,22]
N = 4
BF = ml_dtypes.bfloat16
W, M, H, L, CAP, RO = 2048, 2048, 4096, 256, 48, 4
def sums(w, x):
    return np.add.reduce(w[..., 0:1] * x, axis=2) & 4095, np.add.reduce(w[..., 1:2] * x, axis=2) & 4095
def probe(w, lm, tl, mo, m):
    u, v = sums(w, m); a = (u * v) >> 5
    c = (a[:, :, None] + w[..., 2:3] * u[:, :, None]) & (W - 1)
    x = np.take_along_axis(lm, c.reshape(N, 8, 1, 16 * L), 3).reshape(N, 8, 16, 16, L)
    ok = np.all(x <= m[:, :, :, None], axis=2); has = np.any(ok, axis=2)
    g = np.take_along_axis(c, np.argmax(ok, axis=2)[:, :, None], 2)
    tg = np.take_along_axis(tl, g, 3); q = m - np.take_along_axis(lm, g, 3)
    y = np.take_along_axis(mo, tg.reshape(N, 8, 1, 16 * L), 3).reshape(N, 8, 16, 16, L)
    p = np.minimum(q[:, :, :, None] + y, 255).reshape(N, 8, 16, 16 * L)
    e, f = sums(w, p); h = (((e * f) >> 5) + e) & (H - 1)
    return a, c[:, :, 0], has, tg, p, h
def seek(sn, has, p, h):
    new = np.any(np.take_along_axis(sn, h[:, :, None], 3) != p, axis=2).reshape(N, 8, 16, L) & has[:, :, None]
    return np.any(new, axis=2), np.argmax(new, axis=2)
def first(key):
    o = np.argsort(key, axis=2, kind="stable"); s = np.take_along_axis(key, o, 2)
    b = np.ones(key.shape, bool); b[..., 1:] = s[..., 1:] != s[..., :-1]
    win = np.zeros(key.shape, bool); np.put_along_axis(win, o, b, 2); return win
def turn(st, pr, fill):
    lm, tl, sn, m, ct, ci = st; a, c0, has, tg, p, h = pr
    child, i = seek(sn, has, p, h); j = i * L + np.arange(L)
    pc = np.take_along_axis(p, j[:, :, None], 3); hc = np.take_along_axis(h, j, 2)
    win = first(np.where(child, hc, np.where(has, 2 ** 15 + np.arange(L), 2 ** 14 + c0)))
    wt = np.where(np.arange(16)[:, None] == ci[:, :, None], (a & (M - 1))[:, :, None], ct)
    lm, tl, sn = lm.copy(), tl.copy(), sn.copy()
    for r in range(N):
        for g in range(8):
            b = win[r, g] & child[r, g]; sn[r, g][:, hc[r, g, b]] = pc[r, g][:, b]
            b = win[r, g] & ~has[r, g]; lm[r, g][:, c0[r, g, b]] = m[r, g][:, b]; tl[r, g][:, c0[r, g, b]] = wt[r, g][:, b]
    nm, nt, ni = fill.copy(), tl[..., :L].copy(), np.zeros((N, 8, L), np.int64)
    for d in range(N):
        f = child & ((hc & (N - 1)) == d); f = f & (np.add.accumulate(f.astype(np.int64), axis=2) <= CAP)
        for r in range(N):
            for g in range(8):
                b = np.flatnonzero(f[r, g]); z = r * CAP + np.arange(b.size)
                nm[d, g][:, z] = pc[r, g][:, b]; nt[d, g][:, z] = tg[r, g][:, b]; ni[d, g, z] = i[r, g, b]
    return lm, tl, sn, nm, nt, ni
def mono(rng, n, den, top):
    return ((rng.random((N, 8, 16, n), dtype=np.float32) < den) * rng.integers(1, top + 1, (N, 8, 16, n), dtype=np.int32)).astype(np.int32)
def uneven(rng, n, den):
    v = np.exp2(8 * rng.random((N, 8, 1, n), dtype=np.float32) * rng.random((N, 8, 16, n), dtype=np.float32))
    return ((rng.random((N, 8, 16, n), dtype=np.float32) < den) * np.minimum(v, 255).astype(np.int32)).astype(np.int32)
def base(rng):
    w = np.tile(rng.integers(0, 128, (1, 8, 16, 3), dtype=np.int32), (N, 1, 1, 1)); dens = np.array([0.15, 0.5, 0.8, 1.0, 1.0])
    lm = mono(rng, W, rng.choice(np.array([0.2, 0.3, 0.5]), (N, 8, 1, W)), 160); mo = mono(rng, M, rng.choice(np.array([0.2, 0.4]), (N, 8, 1, M)), 120)
    tl = rng.integers(0, M, (N, 8, 16, W), dtype=np.int32)
    sn = np.where(rng.random((N, 8, 1, H)) < 0.5, -1, mono(rng, H, 0.5, 255)).astype(np.int32)
    m = mono(rng, L, rng.choice(dens, (N, 8, 1, L)), 255); fr = mono(rng, RO * L, rng.choice(dens, (N, 8, 1, RO * L)), 255)
    old = np.take_along_axis(m, rng.integers(0, L, (N, 8, 1, RO * L)), 3)
    return w, lm, tl, mo, sn, m, np.where(rng.random((N, 8, 1, RO * L)) < 0.3, old, fr)
def plant(rng, w, lm, tl, mo, sn, m, fr, until=1, n=L - N * CAP - 8):
    pr = probe(w, lm, tl, mo, m); a, c0, has, tg, p, h = pr; used = np.zeros((N, 8, H), bool)
    cnt = rng.choice(np.array([0, 1, 2, 5, 15, 16]), (N, 8, L), p=[0.5, 0.2, 0.15, 0.05, 0.05, 0.05])
    for r in range(N):
        for g in range(8):
            for k in (1, 2, 5, 15, 16):
                x = np.flatnonzero(has[r, g] & (cnt[r, g] == k)); j = (np.arange(k)[:, None] * L + x).reshape(-1)
                sn[r, g][:, h[r, g, j]] = p[r, g][:, j]; used[r, g, h[r, g, j]] = True
    st = (lm, tl, sn, m, tl[..., :L], np.zeros((N, 8, L), np.int64))
    for t in range(until):
        was, row = st[1], st[5]; st = turn(st, pr, fr[..., t * L:(t + 1) * L])
        pr = probe(w, st[0], st[1], mo, st[3])
    own = pr[0] & (M - 1); came = np.any(st[3] != fr[..., (until - 1) * L:until * L], axis=2)
    stale = ~pr[2] & ~came & (row > 0)
    lone = ~pr[2] & came; anew = ~pr[2] & ~came & ~stale & np.any(st[1][..., :L] != was[..., :L], axis=2)
    used = used | np.any(st[2] != sn, axis=2)
    for r in range(N):
        for g in range(8):
            x = np.flatnonzero(lone[r, g]); v = np.flatnonzero(anew[r, g])[:4]
            s0 = np.flatnonzero(stale[r, g])[:4]
            if x.size + v.size + s0.size == 0: continue
            o = np.concatenate([s0, v, np.resize(x, n - v.size - s0.size)]) if x.size else np.concatenate([s0, v])
            fr[r, g][:, until * L + N * CAP:until * L + N * CAP + o.size] = st[3][r, g][:, o]
            half = rng.random(x.size) < 0.5
            col = np.concatenate([st[4][r, g][:, x][np.arange(16)[:, None] < st[5][r, g, x]],
                own[r, g, x[half]], own[r, g, v]])
            for part, cs in ((True, own[r, g, x[~half]]), (False, col)):
                y = mo[r, g][:, cs]
                e = np.add.reduce(w[r, g, :, 0:1] * y, axis=0) & 4095; f = np.add.reduce(w[r, g, :, 1:2] * y, axis=0) & 4095
                z = (((e * f) >> 5) + e) & (H - 1); b = ~used[r, g, z]
                if part: y = np.where((y == 0) & (rng.random(y.shape) < rng.choice(np.array([0.1, 0.5]), (1, y.shape[1]))), -1, y)
                sn[r, g][:, z[b]] = y[:, b]
def pack(w, lm, tl, mo, sn, m, fr):
    d = {"lm": lm, "tl": tl, "mo": mo, "sn": sn, "fm": m, "fr": fr, "wk": w}
    return {k: np.ascontiguousarray(x.reshape(N, 128, -1)).astype(np.int32) if k in ("tl", "wk") else np.ascontiguousarray(x.reshape(N, 128, -1)).astype(np.float32).astype(BF) for k, x in d.items()}
def setup_inputs(rng):
    s = base(rng); plant(rng, *s); return pack(*s)
def setup_inputs_again(rng):
    w, lm, tl, mo, sn, m, fr = base(rng); w[:, 2, :, 2] = 0; w[:, 3, :, 0] = 0; lm[:, 0] = 255; lm[:, 1] = 0; lm[N - 1, 3, :, 0] = 0; sn[:] = -1
    few = np.tile(rng.integers(0, M, (1, 8, 1, 5), dtype=np.int32), (N, 1, 1, 1))
    tl = np.take_along_axis(few, rng.integers(0, 5, (N, 8, 16, W)), 3); tl[:, :, 7] = rng.integers(0, M, (N, 8, W))
    fr = np.take_along_axis(m, rng.integers(0, 12, (N, 8, 1, RO * L)), 3); m = np.take_along_axis(m, rng.integers(0, 12, (N, 8, 1, L)), 3)
    return pack(w, lm, tl, mo, sn, m, fr)
def setup_inputs_corners(rng):
    w, lm, tl, mo, sn, m, fr = base(rng)
    lm[:, :, 0] = np.where(np.any(lm > 0, axis=2), lm[:, :, 0], 1); tl[:, 5] = rng.choice(np.array([0, M - 1]), (N, 16, W))
    fr[..., ::7] = 0; fr[..., 3::7] = 255
    pool, to = [], []
    for z in range(2):
        x = mono(rng, L, 0.9, 255); pr = probe(w, lm, tl, mo, x); child, i = seek(sn, pr[2], pr[4], pr[5])
        hc = np.take_along_axis(pr[5], i * L + np.arange(L), 2); pool.append(x); to.append(np.where(child, hc & (N - 1), -1))
    pool = np.concatenate(pool, axis=3); to = np.concatenate(to, axis=2)
    for r in range(N):
        for g in range(8):
            left = L; lanes = []
            for e in range(N):
                n = int(rng.choice(np.array([0, 1, CAP - 1, CAP, CAP + 1, 2 * CAP])))
                if r == 0 and e == 0: n = (CAP, CAP + 1, CAP - 1, 0, 1, CAP, CAP + 1, 2 * CAP)[g]
                if r == N - 1 and e == 0: n = CAP
                x = np.flatnonzero(to[r, g] == (r + 1 + e) % N)[:min(n, left)]; lanes.append(x); left -= x.size
            x = np.concatenate(lanes); m[r, g] = 0; m[r, g][:, rng.permutation(L)[:x.size]] = pool[r, g][:, x]
    return pack(w, lm, tl, mo, sn, m, fr)
def setup_inputs_ends(rng):
    def sub(n, den):
        return 255 * (rng.random((N, 8, 16, n)) < den).astype(np.int32)
    w = 127 * rng.integers(0, 2, (8, 16, 3)); w[6, :, 0:2] = 127; w[7, :, 0:2] = 0; w[:, 0, 2] = 0; w[:, 15, 2] = 127
    w[7, 0:4, 0] = 127; w[7, 4:8, 1] = 127; w[7, 13:16, 0] = (127, 127, 3); w[7, 10:13, 1] = (127, 127, 3)
    w = np.tile(w[None], (N, 1, 1, 1)).astype(np.int32); dens = np.array([0.0, 0.3, 0.6, 0.9, 1.0])
    lm = sub(W, 0.15); mo = sub(M, 0.3); tl = (M - 1) * rng.integers(0, 2, (N, 8, 16, W))
    t = rng.integers(0, 3, (N, 8, 1, H)); sn = np.where(t == 0, -1, np.where(t == 1, 255, 256 * rng.integers(0, 2, (N, 8, 16, H)) - 1))
    m = sub(L, rng.choice(dens, (N, 8, 1, L))); fr = sub(RO * L, rng.choice(dens, (N, 8, 1, RO * L)))
    for x in (m, fr):
        x[..., 0] = 255; x[..., -1] = 255
        z = rng.random(x.shape[-1]) < 0.3; z[0] = True; z[-1] = True
        x[:, 7, 0:8][:, :, z] = 0; x[:, 7, 10:16][:, :, z] = 255
    return pack(w, lm, tl, mo, sn, m, fr)
def setup_inputs_late(rng):
    w, lm, tl, mo, sn, m, fr = base(rng)
    lm = mono(rng, W, rng.choice(np.array([0.5, 0.6]), (N, 8, 1, W)), 160)
    pool = mono(rng, 8192, 0.5, 255); u, v = sums(w, pool)
    aim = np.where(np.arange(8) % 2 == 1, H - 1, 0)[:, None]
    k = np.argmax(((((u * v) >> 5) + u) & (H - 1)) == aim, axis=2)
    mo[..., M - 1:] = np.take_along_axis(pool, k[:, :, None, None], 3); sn[..., 0] = -1; sn[..., H - 1] = -1
    x = mono(rng, 4, 0.6, 255); u, v = sums(w, x); c0 = (((u * v) >> 5) + w[:, :, 0, 2:3] * u) & (W - 1)
    np.put_along_axis(lm, c0[:, :, None], x, 3); np.put_along_axis(tl[:, :, 0], c0, M - 1, 2)
    for t in (1, 2):
        fr[..., t * L + N * CAP + 24:t * L + N * CAP + 28] = x
    one = mono(rng, 1, 0.4, 255)
    for g in (3, 4):
        fr[:, g, :, :L] = one[:, g]
    s = (w, lm, tl, mo, sn, m, fr); plant(rng, *s, until=2, n=24); return pack(*s)
def setup_inputs_spread(rng):
    w = np.tile((np.exp2(7 * rng.random((1, 8, 16, 3))) - 1).astype(np.int32), (N, 1, 1, 1)); dens = np.array([0.3, 0.7, 1.0])
    lm = uneven(rng, W, rng.choice(np.array([0.2, 0.4]), (N, 8, 1, W))); mo = uneven(rng, M, 0.4)
    tl = np.minimum(M * rng.random((N, 8, 16, W)) ** 3, M - 1).astype(np.int32); sn = uneven(rng, H, 0.7) - 1
    m = uneven(rng, L, rng.choice(dens, (N, 8, 1, L))); fr = uneven(rng, RO * L, rng.choice(dens, (N, 8, 1, RO * L)))
    s = (w, lm, tl, mo, sn, m, fr); plant(rng, *s); return pack(*s)
def check_inputs(d):
    bad = []
    for k, lo, hi in (("lm", 0, 255), ("tl", 0, M - 1), ("mo", 0, 255), ("sn", -1, 255), ("fm", 0, 255), ("fr", 0, 255), ("wk", 0, 127)):
        x = np.asarray(d[k]).astype(np.float32)
        if not (np.all(x >= lo) and np.all(x <= hi)): bad.append("range of " + k)
        elif np.any(x != np.floor(x)): bad.append("whole numbers in " + k)
    if np.any(d["wk"] != d["wk"][:1]): bad.append("wk alike on all ranks")
    return bad
def reference(lm, tl, mo, sn, fm, fr, wk):
    lead, tail, mon, seen, front, fill, w = [x.astype(np.float32).astype(np.int32).reshape(N, 8, 16, -1) for x in (lm, tl, mo, sn, fm, fr, wk)]
    st = (lead, tail, seen, front, tail[..., :L], np.zeros((N, 8, L), np.int64))
    for t in range(RO):
        st = turn(st, probe(w, st[0], st[1], mon, st[3]), fill[..., t * L:(t + 1) * L])
    return {"yl": st[0].reshape(N, 128, W).astype(np.float32).astype(BF), "yf": st[3].reshape(N, 128, L).astype(np.float32).astype(BF)}

@@ -1,0 +1,571 @@
+from concourse.bass import DstId, RemoteDMATransfer
+from concourse.mybir import AluOpType as A, ActivationFunctionType as F
+
+BF, FP, I32, U16 = "bfloat16", "float32", "int32", "uint16"
+POOLS = {
+    "PLFP": ["LANE", "BASE", "BD", "L1", "L2", "L6", "HASF", "NOH", "VH", "PLF", "S3", "S4", "NN", "NONE", "N8", "CH", "A1", "A2",
+             "A3", "KA", "KH", "WIN", "DD", "NA", "PLB"],
+    "PLI": ["TPR", "TAL", "KK", "KC", "C0T", "C0I", "CPR", "CHH", "DI", "KEY", "CPS"],
+    "PLU": ["GL", "LSEL", "PL", "SLOT", "PL2", "LLa", "LLb"],
+}
+SIZES = {
+    BF: {"TAB": 6400, "MO": 2048, "FR": 1024, "M": 1280, "BLK": 128, "IDN": 128, "Z": 128, "NTR": 128, "ONES": 128, "DK": 128, "WBU": 128,
+         "WBV": 128, "KUH": 128, "KUL": 128, "IDM": 128, "RHK": 256, "JC": 256, "KB": 2, "SEG": 256, "C255": 256, "ZER": 256, "C256": 64,
+         "WU": 2048, "WV": 2048, "VN": 2048, "MS": 2048, "SEL": 2048, "TRI": 2048, "MREF": 192, "MX": 4096, "MXR": 3072, "X": 4096,
+         "MN": 256, "ZQ": 256, "ZX": 4096, "R": 4352, "TT": 4096, "PCB": 256, "E": 64, "CS": 64, "KPB": 32, "EQ": 4096, "DUPS": 256,
+         "VAL": 256, "SM0": 1280, "SM1": 1280, "SM2": 1280, "SM3": 1280},
+    FP: {"TL": 2304, "PF": 4, "WF": 4, "WN": 4, "K0": 1, "CAP": 256, "TRC": 16, "ROW": 16, "SELM": 32, "NBC": 2, "COLF": 32, "SC": 256,
+         "YY": 256, "SL": 64, "S2": 32, "TGF": 256, "SELG": 256, "LT": 768, "NB": 256, "MT": 256, "MK": 256, "MT1": 256, "MT2": 256,
+         "MKA": 256, "KF": 16, "NKF": 16, "EQT": 640, "ST0": 1280, "ST1": 1280, "ST2": 1280},
+    I32: {"TLI": 2048, "WKI": 3, "CI": 256, "CM": 256, "PI": 1, "PR": 1, "PG": 1, "CG": 128, "KWI": 128, "KWT": 128, "UI": 512, "PRD": 256,
+          "AR": 256, "ARF": 192, "CT": 256, "TUI": 32, "HP": 256, "HI": 256, "CUI": 32, "KP": 32},
+    U16: {"LST": 256, "LSTR": 192, "TG": 256, "HL": 256, "KR": 256},
+}
+SCRATCH = {"FL": ("sbuf", [128, 16, 256], BF)}
+for _d in SIZES:
+    for _n in SIZES[_d]:
+        SCRATCH[_n] = ("sbuf", [128, SIZES[_d][_n]], _d)
+for _n, _d in (("PLFP", FP), ("PLI", I32), ("PLU", U16)):
+    SCRATCH[_n] = ("sbuf", [128, 16 * len(POOLS[_n])], _d)
+for _b in range(8):
+    SCRATCH["b%d" % _b] = ("psum", [128, 512], FP)
+_DMAS = ["wk", "fm", "fr", "lm", "tl", "mo", "sn", "yl", "yf"]
+SEMAPHORES = (["sv", "ss", "st", "sg", "loc"] + ["d" + x for x in _DMAS]
+              + ["pre%d" % t for t in range(4)] + ["fm%d" % t for t in range(1, 5)] + ["ft%d" % t for t in range(1, 4)])
+L_S0 = [(10, 12), (12, 14), (14, 16)]
+L_S = [(12, 14), (14, 16), (10, 12), (8, 10)]
+P_S = [(4, 6), (6, 8), (12, 14), (14, 16)]
+S_S = [(6, 8), (4, 6), (14, 16)]
+MX_V, ZX_S, EQ_S = 4, 0, 10
+EST = {"vL": 0.47, "vT": 0.68, "vR": 0.26, "sG": 0.70, "sP": 0.53}
+
+
+def rank_program(g, core, T, topo):
+    rank = T.rank_of(core)
+    if rank is None:
+        return
+    peers = [r for r in range(len(T.cores)) if r != rank]
+    S = T.sem
+    Q = {"v": g.vector, "s": g.scalar, "t": g.tensor, "g": g, "y": g.sync}
+    SN = {"v": "sv", "s": "ss", "t": "st", "g": "sg"}
+    cnt = {k: 0 for k in SEMAPHORES}
+    known = {e: {} for e in Q}
+    snap, wr_, rd_, ps_ = {}, {}, {}, {}
+    P = {}
+    for pn in POOLS:
+        for i, n in enumerate(POOLS[pn]):
+            P[n] = T[pn][:, 16 * i:16 * i + 16]
+
+    def is_bank(k):
+        return k[0] == "b" and k[1:].isdigit()
+
+    def sync(e, toks):
+        need = {}
+        for s, v in toks:
+            if known[e].get(s, 0) < v:
+                need[s] = max(need.get(s, 0), v)
+        drop = [s for s in need if any(s2 != s and snap.get((s2, need[s2]), {}).get(s, 0) >= need[s] for s2 in need)]
+        for s, v in need.items():
+            if s not in drop:
+                Q[e].wait_ge(S[s], v)
+        for s, v in need.items():
+            known[e][s] = max(known[e].get(s, 0), v)
+            for a, b in snap.get((s, v), {}).items():
+                known[e][a] = max(known[e].get(a, 0), b)
+
+    def deps(e, rd, wr):
+        toks = []
+        for k in rd:
+            toks += wr_.get(k, [])
+        for k in wr:
+            toks += wr_.get(k, []) + rd_.get(k, [])
+        for k in list(rd) + list(wr):
+            if is_bank(k):
+                toks += [tk for e2, tk in ps_.get(k, {}).items() if e2 != e]
+        return toks
+
+    def note(e, tok, rd, wr):
+        for k in list(rd) + list(wr):
+            if is_bank(k):
+                ps_.setdefault(k, {})[e] = tok
+        for k in rd:
+            rd_[k] = [x for x in rd_.get(k, []) if x[0] != tok[0]] + [tok]
+        for k in wr:
+            wr_[k], rd_[k] = [tok], []
+
+    def op(e, rd, wr, name, *a, **kw):
+        toks = deps(e, rd, wr)
+        if e == "t":
+            toks = [x for x in toks if x[0] != "st"]
+        sync(e, toks)
+        f = {"cp": lambda: g.vector.tensor_copy, "tt": lambda: g.vector.tensor_tensor, "ts": lambda: g.vector.tensor_scalar,
+             "scan": lambda: g.vector.tensor_tensor_scan, "ms": lambda: g.vector.memset, "act": lambda: g.scalar.activation,
+             "mm": lambda: g.tensor.matmul, "iota": lambda: g.iota}[name]()
+        s = SN[e]
+        cnt[s] += 1
+        f(*a, **kw).then_inc(S[s], 1)
+        snap[(s, cnt[s])] = dict(known[e])
+        note(e, (s, cnt[s]), rd, wr)
+
+    def dma(e, sem, out, in_, rd, wr):
+        sync(e, deps(e, rd, wr))
+        cnt[sem] += 16
+        Q[e].dma_start(out, in_).then_inc(S[sem], 16)
+        snap[(sem, cnt[sem])] = dict(known[e])
+        note(e, (sem, cnt[sem]), rd, wr)
+
+    def V(rd, wr, name, *a):
+        op("v", rd, wr, name, *a)
+
+    def ops(*rows):
+        for r in rows:
+            name, out, ins = r[0], r[1], [x for x in r[2:] if isinstance(x, str)]
+            V(ins, [out], name, *[ap(x) if isinstance(x, str) else x for x in r[1:]])
+
+    def ap(n):
+        return P[n] if n in P else T[n][:]
+
+    def SA(rd, wr, out, in_, fn=F.Copy, **kw):
+        op("s", rd, wr, "act", out, in_, fn, **kw)
+
+    def mm(rd, bank, out, lhsT, rhs, start, stop):
+        op("t", rd, [bank], "mm", out, lhsT, rhs, start, stop)
+
+    def blk(name, r):
+        return T[name][:, 128 * r:128 * (r + 1)]
+
+    def land(key, sem, n=12):
+        cnt[sem] += n
+        wr_[key] = [(sem, cnt[sem])]
+
+    def send(sem, pieces, rd):
+        sync("g", deps("g", rd, []))
+        tr = []
+        for n, p in enumerate(peers):
+            rid, pid, _ = topo.addr(T.cores[p])
+            dst, src = pieces(p)
+            eng = topo.engines(core, T.cores[p])
+            tr.append(RemoteDMATransfer(dst_ids=[DstId(rid=rid, pnc=pid)], dma_engine_mask=sum(1 << x for x in eng[4 * n:4 * n + 4]),
+                                        remote_sem=S[sem], src=src, dst=dst))
+        g.remote_dma_fused(tr, local_sem=S.loc)
+        cnt["loc"] += 12
+        snap[("loc", cnt["loc"])] = dict(known["g"])
+        note("g", ("loc", cnt["loc"]), rd, [])
+
+    for t in range(4):
+        land("SM%dp" % t, "pre%d" % t)
+    for t in range(1, 5):
+        land("M%dr" % t, "fm%d" % t)
+    for t in range(1, 4):
+        land("LT%dr" % t, "ft%d" % t)
+    dma("y", "dwk", T.WKI[:], T.wk[:], [], ["WKI"])
+    dma("s", "dfm", T.M[:, 0:256], T.fm[:], [], ["M0"])
+    dma("s", "dlm", T.TAB[:, 4096:6144], T.lm[:], [], ["LM"])
+    dma("y", "dfr", T.FR[:], T.fr[:], [], ["FR"])
+    dma("y", "dtl", T.TLI[:], T.tl[:], [], ["TLI"])
+    dma("s", "dmo", T.MO[:], T.mo[:], [], ["MO"])
+    dma("y", "dsn", T.TAB[:, 0:4096], T.sn[:], [], ["SN"])
+
+    op("g", [], ["CI"], "iota", T.CI[:], [[1, 256]], 0, 0)
+    op("g", [], ["PI"], "iota", T.PI[:], [[0, 1]], 0, 1)
+    for t in range(4):
+        send("pre%d" % t, lambda p: (T["SM%d" % t][:, 256 * rank:256 * rank + 48], T.FR[:, 256 * t + 48 * p:256 * t + 48 * p + 48]), ["FR"])
+    rp, gp, pf = T.PF[:, 0:1], T.PF[:, 1:2], T.PF[:, 2:3]
+    wc, kc = T.WF[:, 0:1], T.WF[:, 2:3]
+    V([], ["ONES"], "ms", T.ONES[:], 1.0)
+    ops(("ts", "CM", "CI", 15, None, A.bitwise_and), ("ts", "PR", "PI", 15, None, A.bitwise_and), ("ts", "PG", "PI", 4, None, A.arith_shift_right))
+    V(["CI"], ["CG"], "ts", T.CG[:], T.CI[:, 0:128], 4, None, A.arith_shift_right)
+    V(["PR"], ["PF0"], "cp", rp, T.PR[:])
+    V(["PG"], ["PF1"], "cp", gp, T.PG[:])
+    V(["PI"], ["PF2"], "cp", pf, T.PI[:])
+    V(["CG", "PF1"], ["BLK"], "ts", T.BLK[:], T.CG[:], gp, None, A.is_equal)
+    V(["CI", "PF2"], ["IDN"], "ts", T.IDN[:], T.CI[:, 0:128], pf, None, A.is_equal)
+    V(["WKI"], ["WF"], "cp", T.WF[:, 0:3], T.WKI[:])
+    V(["IDN", "WF"], ["DK"], "ts", T.DK[:], T.IDN[:], kc, None, A.mult)
+    mm(["ONES", "DK"], "b0", T.b0[:, 0:128], T.ONES[:], T.DK[:], True, True)
+    V(["BLK", "WF"], ["WBU"], "ts", T.WBU[:], T.BLK[:], wc, None, A.mult)
+    V(["BLK", "WF"], ["WBV"], "ts", T.WBV[:], T.BLK[:], T.WF[:, 1:2], None, A.mult)
+    V(["WKI"], ["WN"], "ts", T.WN[:, 0:3], T.WKI[:], -1.0, None, A.mult)
+    V(["b0", "WF"], ["KWI"], "ts", T.KWI[:], T.b0[:, 0:128], wc, None, A.mult)
+    ops(("ts", "KWT", "KWI", 2040, None, A.bitwise_and), ("tt", "KUH", "KWT", "BLK", A.mult),
+        ("ts", "KWT", "KWI", 7, None, A.bitwise_and), ("tt", "KUL", "KWT", "BLK", A.mult))
+
+    def candidates(n, src, key, lst, lkey, ar, akey):
+        mm(["WBU"] + key, "b0", T.b0[:, 0:n], T.WBU[:], src, True, True)
+        mm(["WBV"] + key, "b0", T.b0[:, n:2 * n], T.WBV[:], src, True, True)
+        mm(["KUH"] + key, "b1", T.b1[:, 0:n], T.KUH[:], src, True, False)
+        mm(["KUL"] + key, "b1", T.b1[:, 0:n], T.KUL[:], src, False, True)
+        V(["b0"], ["UI"], "cp", T.UI[:, 0:2 * n], T.b0[:, 0:2 * n])
+        V(["UI"], ["UI"], "ts", T.UI[:, 0:2 * n], T.UI[:, 0:2 * n], 4095, None, A.bitwise_and)
+        V(["UI"], ["PRD"], "tt", T.PRD[:, 0:n], T.UI[:, 0:n], T.UI[:, n:2 * n], A.mult)
+        V(["PRD"], [akey], "ts", ar, T.PRD[:, 0:n], 5, 2047, A.arith_shift_right, A.bitwise_and)
+        V([akey, "b1"], ["CT"], "tt", T.CT[:, 0:n], ar, T.b1[:, 0:n], A.add)
+        V(["CT"], ["CT"], "ts", T.CT[:, 0:n], T.CT[:, 0:n], 2047, None, A.bitwise_and)
+        V(["CT"], [lkey], "cp", lst, T.CT[:, 0:n])
+
+    for i in range(16):
+        SA(["M0"], ["MX%d" % i], T.MX[:, i::16], T.M[:, 0:256])
+    candidates(256, T.M[:, 0:256], ["M0"], T.LST[:], "LST", T.AR[:], "AR")
+
+    V(["CM"], ["Z"], "ts", T.Z[:], T.CM[:, 0:128], -99.0, None, A.add)
+    ops(("tt", "Z", "Z", "BLK", A.mult), ("ts", "Z", "Z", 99.0, None, A.add))
+    for r in range(16):
+        V(["Z"], ["MS%d" % r], "ts", blk("MS", r), T.Z[:], float(r), None, A.is_equal)
+    MSK = ["MS%d" % r for r in range(16)]
+    V(MSK, ["VN"], "ts", T.VN[:], T.MS[:], -4096.0, None, A.mult)
+    SA(MSK + ["WN"], ["WU"], T.WU[:], T.MS[:], scale=T.WN[:, 0:1])
+    SA(MSK + ["WN"], ["WV"], T.WV[:], T.MS[:], scale=T.WN[:, 1:2])
+    V(["CI", "PF2"], ["IDM"], "ts", T.IDM[:], T.CI[:, 0:128], pf, -1.0, A.is_equal, A.mult)
+    ops(("ts", "SEG", "CM", 0.0, None, A.is_gt), ("ts", "CAP", "CM", -0.0625, 1.0, A.mult, A.add), ("ts", "JC", "CAP", 2048.0, None, A.mult))
+    V(["CM", "PF0", "WF"], ["RHK"], "ts", T.RHK[:], T.CM[:], rp, kc, A.is_equal, A.mult)
+    V([], ["C255"], "ms", T.C255[:], 255.0)
+    V([], ["ZER"], "ms", T.ZER[:], 0.0)
+    V(["TLI"], ["TL"], "cp", T.TL[:, 0:2048], T.TLI[:])
+    V(["M0"], ["MN"], "ts", T.MN[:], T.M[:, 0:256], -1.0, 255.0, A.mult, A.add)
+
+    def constants_2():
+        V(["CI", "PF0"], ["ROW"], "ts", T.ROW[:], T.CI[:, 0:16], rp, None, A.is_equal)
+        V(["CI", "PF0"], ["TRC"], "ts", T.TRC[:], T.CI[:, 0:16], rp, None, A.is_gt)
+        V(["WF"], ["KB"], "cp", T.KB[:], T.WF[:, 1:3])
+        V(["CM", "PF0"], ["NTR"], "ts", T.NTR[:], T.CM[:, 0:128], rp, -1.0, A.is_le, A.mult)
+        ops(("tt", "NTR", "NTR", "BLK", A.mult))
+        V(["CI", "PF0"], ["COLF"], "ts", T.COLF[:], T.CI[:, 0:32], rp, None, A.add)
+        ops(("ts", "SELM", "COLF", 16.0, 12288.0, A.is_equal, A.mult))
+        V(["CI"], ["LANE"], "ts", P["LANE"], T.CI[:, 0:16], 16.0, None, A.mult)
+        V(["LANE", "PF0"], ["LANE"], "ts", P["LANE"], P["LANE"], rp, None, A.add)
+        ops(("ts", "BASE", "LANE", 16.0, 16.0, A.mult, A.add), ("ts", "BD", "LANE", -15.0, 4080.0, A.mult, A.add),
+            ("ts", "L1", "LANE", 1024.0, None, A.add), ("ts", "L2", "LANE", 2048.0, None, A.add), ("ts", "L6", "LANE", 6144.0, None, A.add))
+        V(["PF0"], ["NBC0"], "ts", T.NBC[:, 0:1], rp, 0.0, None, A.is_gt)
+        V(["PF0"], ["NBC1"], "ts", T.NBC[:, 1:2], rp, 0.0, 4096.0, A.is_equal, A.mult)
+        for d in range(4):
+            V([], ["C256_%d" % d], "ms", T.C256[:, 16 * d:16 * d + 16], 256.0 * d)
+        for t in range(3):
+            V(["FR"], ["MREF%d" % t], "cp", T.MREF[:, 64 * t:64 * t + 64], T.FR[:, 256 * t + 192:256 * t + 256])
+
+    def constants_s():
+        for t in range(4):
+            SA(["FR"], ["M%df" % (t + 1)], T.M[:, 256 * t + 448:256 * t + 512], T.FR[:, 256 * t + 192:256 * t + 256])
+            SA(["FR"], ["SM%do" % t], T["SM%d" % t][:, 256 * rank:256 * rank + 48], T.FR[:, 256 * t + 48 * rank:256 * t + 48 * rank + 48])
+        for t in range(3):
+            SA(["ZER"], ["LT%df" % (t + 1)], T.LT[:, 256 * t + 192:256 * t + 256], T.ZER[:, 0:64])
+            for d in range(4):
+                SA(["ZER"], ["ST%d_%d" % (t, d)], T["ST%d" % t][:, 256 * d:256 * d + 48], T.ZER[:, 0:48])
+        for r in range(16):
+            SA(["BLK", "ROW"], ["SEL%d" % r], blk("SEL", r), T.BLK[:], scale=T.ROW[:, r:r + 1])
+        for r in range(16):
+            SA(["MS%d" % r, "TRC"], ["TRI%d" % r], blk("TRI", r), blk("MS", r), scale=T.TRC[:, r:r + 1])
+        mm(["SEL0", "KB"], "b2", T.b2[:, 0:1], blk("SEL", 0), T.KB[:, 1:2], True, True)
+        V(["b2"], ["K0"], "cp", T.K0[:], T.b2[:, 0:1])
+    C256K = ["C256_%d" % d for d in range(4)]
+    MRK = ["MREF0", "MREF1", "MREF2"]
+
+    def merge(a, b):
+        ta = tb = 0.0
+        a, b = list(a), list(b)
+        while a or b:
+            if b and (not a or tb + b[0][0] <= ta + a[0][0]):
+                tb += b[0][0]
+                b.pop(0)[1]()
+            else:
+                ta += a[0][0]
+                a.pop(0)[1]()
+
+    def pipe(chunks, gather, diff, post, after):
+        out, n = [], len(chunks)
+
+        def g1(k):
+            gather(chunks[k])
+            diff(chunks[k], "b%d" % (5 + k % 2))
+
+        def p1(k):
+            post(chunks[k], "b%d" % (5 + k % 2))
+            after(chunks[k])
+        for k in range(n + 1):
+            if k < n:
+                out.append((EST["sG"], lambda k=k: g1(k)))
+            if k > 0:
+                out.append((EST["sP"], lambda k=k: p1(k - 1)))
+        return out
+
+    def share(sc):
+        vp = [(c, c + 2) for c in range(0, 16, 2) if (c, c + 2) not in sc]
+        ends, k = {}, 0
+        while k < len(vp):
+            j = k + 1 if k + 1 < len(vp) and vp[k + 1][0] == vp[k][1] else k
+            ends[vp[j][1] - 1] = vp[k][0]
+            k = j + 1
+        return vp, ends
+
+    def sums(bank, sel, c0, c1, state):
+        state[0] += c1 - c0
+        for r in range(16):
+            mm(["FL%d" % c for c in range(c0, c1)] + ([sel] if sel == "VN" else ["MS%d" % r]), bank, T[bank][:, 16 * c0:16 * c1], blk(sel, r),
+               T.FL[:, c0:c1, 16 * r:16 * r + 16], False, bool(state[0] == 16 and r == 15))
+
+    LM, SNW = T.TAB[:, 4096:6144], T.TAB[:, 0:4096]
+    MXK, ZXK = ["MX%d" % i for i in range(16)], ["ZX%d" % i for i in range(16)]
+    RK = ["R%d" % c for c in range(16)] + ["Rm"]
+
+    for t in range(4):
+        m = T.M[:, 256 * t:256 * t + 256]
+        nx = 256 * (t + 1)
+        mk = ["M0"] if t == 0 else ["M%d%s" % (t, x) for x in "rof"]
+        LS = L_S if t else L_S0
+
+        def lsrc(c0, c1):
+            if t and c0 >= 12:
+                o = 64 * (t - 1) + 16 * (c0 - 12)
+                return (T.LSTR[:, o:o + 16 * (c1 - c0)], T.MXR[:, 16 * o:16 * o + 256 * (c1 - c0)], ["LSTR"], ["MXR"])
+            return (T.LST[:, 16 * c0:16 * c1], T.MX[:, 256 * c0:256 * c1], ["LST"], MXK)
+
+        def lgather(ch):
+            o, mx, k1, k2 = lsrc(*ch)
+            SA(["LM"] + k1, ["X%d" % ch[0]], T.X[:, 256 * ch[0]:256 * ch[1]], LM.indirect(o))
+
+        def ldiff(ch, b):
+            o, mx, k1, k2 = lsrc(*ch)
+            mm(["IDN", "X%d" % ch[0]], b, T[b][:], T.IDN[:], T.X[:, 256 * ch[0]:256 * ch[1]], True, False)
+            mm(["IDM"] + k2, b, T[b][:], T.IDM[:], mx, False, True)
+
+        def lpost(ch, b):
+            for c in range(ch[0], ch[1]):
+                o = 256 * (c - ch[0])
+                SA([b], ["FL%d" % c], T.FL[:, c, :], T[b][:, o:o + 256], F.Relu)
+        mm(["BLK", "RHK"], "b3", T.b3[:, 0:256], T.BLK[:], T.RHK[:], True, False)
+        mm(["IDN", "JC"], "b3", T.b3[:, 0:256], T.IDN[:], T.JC[:], False, False)
+        lst8 = [0]
+        vp, ends = share(LS)
+        st = pipe(LS, lgather, ldiff, lpost, lambda ch: sums("b3", "VN", ch[0], ch[1], lst8))
+        if t:
+            candidates(192, T.M[:, 256 * t:256 * t + 192], mk[:2], T.LST[:, 0:192], "LST", T.AR[:, 0:192], "AR")
+            for k in range(3):
+                st.pop(0)[1]()
+            for i in range(16):
+                if i >= MX_V:
+                    SA(mk[:2], ["MX%d" % i], T.MX[:, i:3072:16], T.M[:, 256 * t:256 * t + 192])
+            for i in range(MX_V):
+                V(mk[:2], ["MX%d" % i], "cp", T.MX[:, i:3072:16], T.M[:, 256 * t:256 * t + 192])
+        for k, w in ((0, "WU"), (16, "WV")):
+            for r in range(16):
+                mm([w] + mk, "b2", T.b2[:, k:k + 16], blk(w, r), T.M[:, 256 * t + r:256 * t + 256:16], r == 0, r == 15)
+        vt = []
+        for c in [c for p in vp for c in range(*p)]:
+            def lv(c=c):
+                o, mx, k1, k2 = lsrc(c, c + 1)
+                V(["LM"] + k1 + k2, ["FL%d" % c], "tt", T.FL[:, c, :], LM.indirect(o), mx, A.is_gt)
+                if c in ends:
+                    sums("b3", "VN", ends[c], c + 1, lst8)
+            vt.append((EST["vL"], lv))
+        merge(vt, st)
+        V(["b2"], ["TUI"], "ts", T.TUI[:], T.b2[:, 0:32], -1.0, None, A.mult)
+        ops(("ts", "TUI", "TUI", 4095, None, A.bitwise_and))
+        V(["TUI"], ["TPR"], "tt", P["TPR"], T.TUI[:, 0:16], T.TUI[:, 16:32], A.mult)
+        ops(("ts", "TAL", "TPR", 5, 2047, A.arith_shift_right, A.bitwise_and))
+        if t == 0:
+            constants_2()
+            candidates(192, T.MREF[:], MRK, T.LSTR[:], "LSTR", T.ARF[:], "ARF")
+            SA(["SN"], ["SN"], T.TAB[:, 0:4096], T.TAB[:, 0:4096], F.Identity, bias=255.0, scale=-1.0)
+        V(["SEG", "b3"], ["SC"], "scan", T.SC[:], T.SEG[:], T.b3[:, 0:256], 0.0, A.mult, A.max)
+        V(["SC"], ["KK"], "cp", P["KK"], T.SC[:, 15::16])
+        ops(("ts", "KK", "KK", 127, None, A.bitwise_and))
+        V(["KK", "TUI"], ["KC"], "tt", P["KC"], P["KK"], T.TUI[:, 0:16], A.mult)
+        ops(("tt", "KC", "KC", "TAL", A.add), ("ts", "KC", "KC", 2047, None, A.bitwise_and), ("cp", "GL", "KC"))
+        V(["TL", "GL"], ["TG"], "cp", T.TG[:], T.TL[:, 0:2048].indirect(P["GL"]))
+        V(["LM", "GL", "MN"], ["ZQ"], "tt", T.ZQ[:], LM.indirect(P["GL"]), T.MN[:], A.add)
+        SA(mk, ["Rm"], T.R[:, 4096:4352], m)
+        for i in range(16):
+            if i < ZX_S:
+                SA(["ZQ"], ["ZX%d" % i], T.ZX[:, i::16], T.ZQ[:])
+            else:
+                V(["ZQ"], ["ZX%d" % i], "cp", T.ZX[:, i::16], T.ZQ[:])
+        for b in ("b0", "b1"):
+            mm(["IDN", "ZER"], b, T[b][:, 0:256], T.IDN[:], T.ZER[:], True, False)
+            mm(["WBU", "C255"], b, T[b][:, 0:128], T.WBU[:], T.C255[:, 0:128], False, False)
+            mm(["WBV", "C255"], b, T[b][:, 128:256], T.WBV[:], T.C255[:, 0:128], False, False)
+        nh, done = [0, 0], {}
+
+        def hsum(ch):
+            done[ch[0]] = True
+            k = ch[0] // 4 * 4
+            if not (k in done and k + 2 in done):
+                return
+            c0, c1, h = k, k + 4, k // 8
+            b, l0, n = "b%d" % h, 16 * c0 - 128 * h, 64
+            nh[h] += 4
+            for o, w in ((0, "WU"), (128, "WV")):
+                for i in range(16):
+                    mm(["R%d" % c for c in range(c0, c1)] + [w], b, T[b][:, o + l0:o + l0 + n], blk(w, i),
+                       T.R[:, 256 * c0 + i:256 * c1:16], False, bool(nh[h] == 8 and o and i == 15))
+
+        def pgather(ch):
+            SA(["MO", "TG"], ["X%d" % ch[0]], T.X[:, 256 * ch[0]:256 * ch[1]], T.MO[:].indirect(T.TG[:, 16 * ch[0]:16 * ch[1]]))
+
+        def pdiff(ch, b):
+            mm(["IDN", "X%d" % ch[0]], b, T[b][:], T.IDN[:], T.X[:, 256 * ch[0]:256 * ch[1]], True, False)
+            mm(["IDM"] + ZXK, b, T[b][:], T.IDM[:], T.ZX[:, 256 * ch[0]:256 * ch[1]], False, True)
+
+        def ppost(ch, b):
+            SA([b], ["R%d" % c for c in range(*ch)], T.R[:, 256 * ch[0]:256 * ch[1]], T[b][:], F.Relu, scale=-1.0)
+        vt = []
+        for ch in share(P_S)[0]:
+            def pv1(ch=ch):
+                c0, c1 = ch
+                V(["MO", "TG"] + ZXK, ["TT%d" % c0], "tt", T.TT[:, 256 * c0:256 * c1], T.MO[:].indirect(T.TG[:, 16 * c0:16 * c1]),
+                  T.ZX[:, 256 * c0:256 * c1], A.subtract)
+
+            def pv2(ch=ch):
+                c0, c1 = ch
+                V(["TT%d" % c0], ["R%d" % c for c in range(c0, c1)], "ts", T.R[:, 256 * c0:256 * c1], T.TT[:, 256 * c0:256 * c1], -1.0, 0.0, A.mult, A.max)
+                hsum(ch)
+            vt += [(EST["vT"], pv1), (EST["vR"], pv2)]
+        vt[0] = (EST["vT"] + 0.1 * (16 - ZX_S), vt[0][1])
+        st = pipe(P_S, pgather, pdiff, ppost, hsum)
+        if t == 0:
+            for i in range(16):
+                SA(MRK, ["MXR%d" % i], T.MXR[:, i::16], T.MREF[:])
+            wr_["MXR"] = wr_["MXR15"]
+            constants_s()
+        merge(vt, st)
+        if t < 3:
+            SA(["TL", "GL"], ["TGF"], T.TGF[:], T.TL[:, 0:2048].indirect(P["GL"]), F.Identity, bias=8192.0)
+            SA(["TL", "NBC0", "NBC1"], ["NB"], T.NB[:], T.TL[:, 0:256], F.Identity, bias=T.NBC[:, 1:2], scale=T.NBC[:, 0:1])
+
+        def hashes(h):
+            b = "b%d" % h
+            o = slice(128 * h, 128 * h + 128)
+            V([b], ["UI"], "cp", T.UI[:, 0:256], T[b][:, 0:256])
+            V(["UI"], ["UI"], "ts", T.UI[:, 0:256], T.UI[:, 0:256], 4095, None, A.bitwise_and)
+            V(["UI"], ["PRD"], "tt", T.PRD[:, 0:128], T.UI[:, 0:128], T.UI[:, 128:256], A.mult)
+            V(["PRD"], ["HP"], "ts", T.HP[:, o], T.PRD[:, 0:128], 5, None, A.arith_shift_right)
+            V(["HP", b], ["HP"], "tt", T.HP[:, o], T.HP[:, o], T[b][:, 0:128], A.add)
+            V(["HP"], ["HI"], "ts", T.HI[:, o], T.HP[:, o], 4095, None, A.bitwise_and)
+            V(["HI"], ["HL%d" % h], "cp", T.HL[:, o], T.HI[:, o])
+        hashes(0)
+        mm(["IDN", "ZER"], "b4", T.b4[:, 0:256], T.IDN[:], T.ZER[:], True, False)
+        sst = [0]
+
+        def sgather(ch):
+            SA(["SN", "HL%d" % (ch[0] // 8)], ["X%d" % ch[0]], T.X[:, 256 * ch[0]:256 * ch[1]], SNW.indirect(T.HL[:, 16 * ch[0]:16 * ch[1]]))
+
+        def sdiff(ch, b):
+            mm(["IDN", "X%d" % ch[0]], b, T[b][:], T.IDN[:], T.X[:, 256 * ch[0]:256 * ch[1]], True, False)
+            mm(["IDM"] + ["R%d" % c for c in range(*ch)], b, T[b][:], T.IDM[:], T.R[:, 256 * ch[0]:256 * ch[1]], False, True)
+
+        def spost(ch, b):
+            for c in range(ch[0], ch[1]):
+                o = 256 * (c - ch[0])
+                SA([b], ["FL%d" % c], T.FL[:, c, :], T[b][:, o:o + 256], F.Square)
+        vp, ends = share(S_S)
+        vt = []
+        for c in [c for p in vp for c in range(*p)]:
+            def sv(c=c, ends=ends):
+                V(["SN", "HL%d" % (c // 8), "R%d" % c], ["FL%d" % c], "tt", T.FL[:, c, :], SNW.indirect(T.HL[:, 16 * c:16 * c + 16]),
+                  T.R[:, 256 * c:256 * c + 256], A.not_equal)
+                if c in ends:
+                    sums("b4", "MS", ends[c], c + 1, sst)
+            vt.append((EST["vL"], sv))
+        vt.insert(2, (1.3, lambda: hashes(1)))
+        merge(vt, pipe(S_S, sgather, sdiff, spost, lambda ch: sums("b4", "MS", ch[0], ch[1], sst)))
+        V(["SC"], ["HASF"], "ts", P["HASF"], T.SC[:, 15::16], 128.0, 16.0, A.is_ge, A.mult)
+        V(["SC"], ["NOH"], "ts", P["NOH"], T.SC[:, 15::16], 128.0, None, A.is_lt)
+        V(["b4", "CAP"], ["YY"], "tt", T.YY[:], T.b4[:, 0:256], T.CAP[:], A.min)
+        V(["YY", "SEG"], ["SC"], "scan", T.SC[:], T.SEG[:], T.YY[:], 0.0, A.mult, A.max)
+        V(["SC", "HASF"], ["VH"], "tt", P["VH"], T.SC[:, 15::16], P["HASF"], A.mult)
+        ops(("tt", "PLF", "BASE", "VH", A.subtract), ("cp", "PL", "PLF"))
+        SA(["PL"] + RK, ["PCB"], T.PCB[:], T.R[:].indirect(P["PL"]), F.Identity, bias=255.0, scale=-1.0)
+        for k, w in ((0, "WU"), (16, "WV")):
+            for r in range(16):
+                mm([w, "PCB"], "b2", T.b2[:, k:k + 16], blk(w, r), T.PCB[:, r::16], r == 0, r == 15)
+        ops(("cp", "LSEL", "VH"))
+        if t < 3:
+            src = T.NB
+            sk = ["NB"]
+            if t:
+                V(["NB", "LT%dr" % t, "LT%do" % t, "LT%df" % t], ["MT"], "tt", T.MT[:], T.LT[:, 256 * t - 256:256 * t], T.NB[:], A.max)
+                src, sk = T.MT, ["MT"]
+            SA(["LSEL", "SELM"], ["SELG"], T.SELG[:], T.SELM[:].indirect(P["LSEL"]))
+            SA(sk, ["MT1"], T.MT1[:], src[:], F.Abs, bias=-8192.0)
+            SA(["MT1"], ["MT1"], T.MT1[:], T.MT1[:], F.Abs, bias=-4096.0)
+            SA(["MT1"], ["MK"], T.MK[:], T.MT1[:], F.Relu, bias=1.0, scale=-1.0)
+            SA(["MT1"], ["MT1"], T.MT1[:], T.MT1[:], F.Abs, bias=-2048.0)
+            SA(["MT1"], ["MT2"], T.MT2[:], T.MT1[:], F.Identity, bias=2048.0, scale=-1.0)
+        ops(("ts", "NONE", "VH", 0.0, None, A.is_equal), ("ts", "CH", "VH", 0.0, None, A.is_gt), ("ts", "N8", "VH", 0.0, 8.0, A.is_equal, A.mult),
+            ("tt", "NN", "NONE", "L1", A.mult), ("tt", "A3", "NONE", "L6", A.mult))
+        V(["TUI", "K0"], ["C0T"], "ts", P["C0T"], T.TUI[:, 0:16], T.K0[:], None, A.mult)
+        ops(("tt", "NA", "NOH", "BD", A.mult), ("tt", "C0T", "C0T", "TAL", A.add), ("tt", "PLB", "NA", "PLF", A.add),
+            ("ts", "C0I", "C0T", 2047, None, A.bitwise_and), ("cp", "PL2", "PLB"), ("tt", "A1", "C0I", "L2", A.subtract),
+            ("tt", "A2", "A1", "NOH", A.mult), ("tt", "KA", "A2", "A3", A.add))
+        SA(["PL2"] + RK, ["VAL"], T.VAL[:], T.R[:].indirect(P["PL2"]))
+        V(["b2"], ["CUI"], "ts", T.CUI[:], T.b2[:, 0:32], -1.0, None, A.mult)
+        ops(("ts", "CUI", "CUI", 4095, None, A.bitwise_and))
+        V(["CUI"], ["CPR"], "tt", P["CPR"], T.CUI[:, 0:16], T.CUI[:, 16:32], A.mult)
+        ops(("ts", "CPR", "CPR", 5, None, A.arith_shift_right))
+        V(["CPR", "CUI"], ["CPS"], "tt", P["CPS"], P["CPR"], T.CUI[:, 0:16], A.add)
+        ops(("ts", "DI", "CPS", 3, None, A.bitwise_and), ("tt", "DD", "DI", "N8", A.add))
+        for d in range(4):
+            V(["DD"], ["E%d" % d], "ts", T.E[:, 16 * d:16 * d + 16], P["DD"], float(d), None, A.is_equal)
+        EK = ["E%d" % d for d in range(4)]
+        mm(["IDN"] + C256K, "b7", T.b7[:, 64:128], T.IDN[:], T.C256[:], True, False)
+        mm(["NTR"] + EK, "b7", T.b7[:, 64:128], T.NTR[:], T.E[:], False, False)
+        V(["SEG"] + EK, ["CS"], "scan", T.CS[:], T.SEG[:, 0:64], T.E[:], 0.0, A.mult, A.add)
+        mm(["BLK", "CS"], "b7", T.b7[:, 64:128], T.BLK[:], T.CS[:], False, True)
+        ops(("ts", "CHH", "CPS", 4095, None, A.bitwise_and), ("tt", "KH", "CHH", "CH", A.mult), ("tt", "KEY", "KH", "KA", A.add))
+        V(["b7"] + EK, ["SL"], "tt", T.SL[:], T.b7[:, 64:128], T.E[:], A.mult)
+        V(["SL"], ["S2"], "tt", T.S2[:], T.SL[:, 0:32], T.SL[:, 32:64], A.add)
+        V(["S2"], ["S3"], "tt", P["S3"], T.S2[:, 0:16], T.S2[:, 16:32], A.add)
+        ops(("tt", "S4", "S3", "NN", A.add), ("cp", "SLOT", "S4"))
+        sm = T["SM%d" % t]
+        V(["SLOT", "PCB", "SM%dp" % t, "SM%do" % t], ["SM%d" % t], "cp", sm[:].indirect(P["SLOT"]), T.PCB[:])
+        send("fm%d" % (t + 1), lambda p: (T.M[:, nx + 48 * rank:nx + 48 * rank + 48], sm[:, 256 * p:256 * p + 48]), ["SM%d" % t])
+        SA(["SM%d" % t], ["M%do" % (t + 1)], T.M[:, nx + 48 * rank:nx + 48 * rank + 48], sm[:, 256 * rank:256 * rank + 48])
+        V(["KEY"], ["KPa"], "ts", T.KP[:, 0:16], P["KEY"], 8160, None, A.bitwise_and)
+        V(["KEY"], ["KPb"], "ts", T.KP[:, 16:32], P["KEY"], 31, None, A.bitwise_and)
+        V(["KPa", "KPb"], ["KPB"], "cp", T.KPB[:], T.KP[:])
+        V(["KEY"], ["NKF"], "ts", T.NKF[:], P["KEY"], -1.0, None, A.mult)
+        for r in range(16):
+            mm(["SEL%d" % r, "KPB"], "b3", T.b3[:, r:256:16], blk("SEL", r), T.KPB[:, 0:16], True, False)
+            mm(["SEL%d" % r, "KPB"], "b3", T.b3[:, r:256:16], blk("SEL", r), T.KPB[:, 16:32], False, True)
+        ops(("cp", "KF", "KEY"))
+        if t < 3:
+            stt = T["ST%d" % t]
+            V(["SLOT", "SELG", "TGF"] + ["ST%d_%d" % (t, d) for d in range(4)], ["ST%d" % t], "tt", stt[:].indirect(P["SLOT"]), T.SELG[:], T.TGF[:], A.max)
+            send("ft%d" % (t + 1), lambda p: (T.LT[:, 256 * t + 48 * rank:256 * t + 48 * rank + 48], stt[:, 256 * p:256 * p + 48]), ["ST%d" % t])
+        V(["b3"], ["KR"], "cp", T.KR[:], T.b3[:, 0:256])
+        off = 0
+        for c in range(EQ_S, 16):
+            n = 256 - 16 * c
+            SA(["b3", "NKF"], ["EQT%d" % c], T.EQT[:, off:off + n], T.b3[:, 16 * c:256], F.Abs, bias=T.NKF[:, c:c + 1])
+            SA(["EQT%d" % c], ["EQ%d" % c], T.EQ[:, 272 * c:256 * c + 256], T.EQT[:, off:off + n], F.Relu, bias=1.0, scale=-1.0)
+            off += n
+        if t < 3:
+            SA(["ST%d" % t], ["LT%do" % (t + 1)], T.LT[:, 256 * t + 48 * rank:256 * t + 48 * rank + 48], stt[:, 256 * rank:256 * rank + 48])
+        mm(["IDN", "ZER"], "b4", T.b4[:, 0:256], T.IDN[:], T.ZER[:], True, False)
+        for c in list(range(EQ_S)) + list(range(EQ_S, 16)):
+            if c < EQ_S:
+                V(["KR", "KF"], ["EQ%d" % c], "ts", T.EQ[:, 272 * c:256 * c + 256], T.KR[:, 16 * c:256], T.KF[:, c:c + 1], None, A.is_equal)
+            if c < 15:
+                mm(["BLK", "EQ%d" % c], "b4", T.b4[:, 16 * c + 16:256], T.BLK[:], T.EQ[:, 272 * c + 16:256 * c + 256], False, c == 14)
+        SA(["b4"], ["DUPS"], T.DUPS[:], T.b4[:, 0:256])
+        EQK = ["EQ%d" % c for c in range(16)]
+        if t == 0:
+            V(["MK", "AR"], ["MKAa", "MKAb"], "tt", T.MKA[:], T.MK[:], T.AR[:], A.mult)
+        elif t < 3:
+            V(["MK", "AR"], ["MKAa"], "tt", T.MKA[:, 0:192], T.MK[:, 0:192], T.AR[:, 0:192], A.mult)
+            V(["MK", "ARF"], ["MKAb"], "tt", T.MKA[:, 192:256], T.MK[:, 192:256], T.ARF[:, 64 * t - 64:64 * t], A.mult)
+        for r in range(16):
+            mm(["TRI%d" % r] + EQK, "b7", T.b7[:, 128:144], blk("TRI", r), T.EQ[:, r::272], r == 0, False)
+        for r in range(16):
+            mm(["MS%d" % r, "DUPS"], "b7", T.b7[:, 128:144], blk("MS", r), T.DUPS[:, r::16], False, r == 15)
+        V(["KF", "L6"], ["A1"], "tt", P["A1"], T.KF[:], P["L6"], A.subtract)
+        V(["b7"], ["WIN"], "ts", P["WIN"], T.b7[:, 128:144], 0.0, None, A.is_equal)
+        ops(("tt", "A2", "A1", "WIN", A.mult), ("tt", "A3", "A2", "L6", A.add), ("cp", "LLa", "A3"))
+        V(["LLa", "VAL"], ["LM", "SN"], "cp", T.TAB[:].indirect(P["LLa"]), T.VAL[:])
+        if t < 3:
+            ops(("tt", "A1", "A2", "NOH", A.mult), ("tt", "A3", "A1", "L2", A.add), ("cp", "LLb", "A3"))
+            V(["LLb", "MT2", "MKAa", "MKAb"], ["TL"], "tt", T.TL[:].indirect(P["LLb"]), T.MT2[:], T.MKA[:], A.max)
+            V(["M%d%s" % (t + 1, x) for x in "rof"], ["MN"], "ts", T.MN[:], T.M[:, nx:nx + 256], -1.0, 255.0, A.mult, A.add)
+    dma("y", "dyl", T.yl[:], T.TAB[:, 4096:6144], ["LM"], [])
+    dma("s", "dyf", T.yf[:], T.M[:, 1024:1280], ["M4r", "M4o", "M4f"], [])
+    for s in SEMAPHORES:
+        if cnt[s] and known["y"].get(s, 0) < cnt[s]:
+            g.sync.wait_ge(S[s], cnt[s])

@@ -16,7 +16,7 @@ SIZES = {
          "VAL": 256, "SM0": 1280, "SM1": 1280, "SM2": 1280, "SM3": 1280},
     FP: {"TL": 2304, "PF": 4, "WF": 4, "WN": 4, "K0": 1, "CAP": 256, "TRC": 16, "ROW": 16, "SELM": 32, "NBC": 2, "COLF": 32, "SC": 256,
          "YY": 256, "SL": 64, "S2": 32, "TGF": 256, "SELG": 256, "LT": 768, "NB": 256, "MT": 256, "MK": 256, "MT1": 256, "MT2": 256,
-         "MKA": 256, "KF": 16, "NKF": 16, "EQT": 640, "ST0": 1280, "ST1": 1280, "ST2": 1280},
+         "MKA": 256, "KF": 16, "NKF": 16, "EQT": 1280, "ST0": 1280, "ST1": 1280, "ST2": 1280},
     I32: {"TLI": 2048, "WKI": 3, "CI": 256, "CM": 256, "PI": 1, "PR": 1, "PG": 1, "CG": 128, "KWI": 128, "KWT": 128, "UI": 512, "PRD": 256,
           "AR": 256, "ARF": 192, "CT": 256, "TUI": 32, "HP": 256, "HI": 256, "CUI": 32, "KP": 32},
     U16: {"LST": 256, "LSTR": 192, "TG": 256, "HL": 256, "KR": 256},
@@ -29,15 +29,24 @@ for _n, _d in (("PLFP", FP), ("PLI", I32), ("PLU", U16)):
     SCRATCH[_n] = ("sbuf", [128, 16 * len(POOLS[_n])], _d)
 for _b in range(8):
     SCRATCH["b%d" % _b] = ("psum", [128, 512], FP)
-_DMAS = ["wk", "fm", "fr", "lm", "tl", "mo", "sn", "yl", "yf"]
+_DMAS = ["wk", "fm", "fr", "lm", "tl", "mo", "sn", "rf", "yl", "yf"]
 SEMAPHORES = (["sv", "ss", "st", "sg", "loc"] + ["d" + x for x in _DMAS]
               + ["pre%d" % t for t in range(4)] + ["fm%d" % t for t in range(1, 5)] + ["ft%d" % t for t in range(1, 4)])
-L_S0 = [(10, 12), (12, 14), (14, 16)]
-L_S = [(12, 14), (14, 16), (10, 12), (8, 10)]
+L_S0 = [(12, 14), (14, 16), (8, 10)]
+L_S = [(12, 14), (14, 16), (8, 10)]
 P_S = [(4, 6), (6, 8), (12, 14), (14, 16)]
-S_S = [(6, 8), (4, 6), (14, 16)]
-MX_V, ZX_S, EQ_S = 4, 0, 10
+P_V = [(0, 4), (8, 12)]
+S_S = [(4, 6), (6, 8), (14, 16)]
+ZX_S, EQ_S = 4, 10
 EST = {"vL": 0.47, "vT": 0.68, "vR": 0.26, "sG": 0.70, "sP": 0.53}
+
+US = {"v": {"FL": 0.45, "TT": 1.35, "R": 0.48, "ZX": 0.16, "UI": 0.3, "PRD": 0.28, "AR": 0.2, "CT": 0.2, "LST": 0.2, "LSTR": 0.2, "SC": 0.26,
+            "YY": 0.26, "TG": 0.42, "ZQ": 0.42, "SM": 0.9, "ST": 0.9, "LM": 0.9, "TL": 1.3, "MT": 0.45, "MKAa": 0.4, "KR": 0.26, "EQ": 0.12,
+            "VN": 0.9, "ARF": 0.2, "HP": 0.15, "HI": 0.15, "HL": 0.15},
+      "s": {"X": 0.72, "FL": 0.26, "R": 0.48, "MX": 0.21, "MXR": 0.21, "ZX": 0.26, "WU": 1.75, "WV": 1.75, "SN": 3.4, "TGF": 0.42, "NB": 0.26,
+            "PCB": 0.42, "SELG": 0.42, "VAL": 0.42, "MT": 0.26, "MK": 0.26, "DUPS": 0.26, "MN": 0.26, "Rm": 0.26, "EQT": 0.13}}
+LOADED = {"dlm": 6.0, "dtl": 10.0, "dmo": 13.0, "dfr": 14.0, "dsn": 18.0, "drf": 19.0}
+WINDOW, WAKE = {"v": 60, "s": 4, "t": 60, "g": 1, "y": 1}, 0.1
 
 
 def rank_program(g, core, T, topo):
@@ -73,46 +82,91 @@ def rank_program(g, core, T, topo):
             for a, b in snap.get((s, v), {}).items():
                 known[e][a] = max(known[e].get(a, 0), b)
 
-    def deps(e, rd, wr):
-        toks = []
-        for k in rd:
-            toks += wr_.get(k, [])
-        for k in wr:
-            toks += wr_.get(k, []) + rd_.get(k, [])
-        for k in list(rd) + list(wr):
-            if is_bank(k):
-                toks += [tk for e2, tk in ps_.get(k, {}).items() if e2 != e]
-        return toks
+    rec = []
 
-    def note(e, tok, rd, wr):
+    def add(e, sem, inc, rd, wr, cost, late, call):
+        n, before, order = len(rec), set(), set()
         for k in list(rd) + list(wr):
             if is_bank(k):
-                ps_.setdefault(k, {})[e] = tok
-        for k in rd:
-            rd_[k] = [x for x in rd_.get(k, []) if x[0] != tok[0]] + [tok]
+                cur = ps_.setdefault(k, [None, [], []])
+                if cur[0] != e:
+                    ps_[k] = cur = [e, [], cur[1]]
+                before.update(cur[2])
+                if e == "t":
+                    order.update(cur[1][-1:])
+                cur[1].append(n)
+            elif k in rd:
+                before.update(wr_.get(k, []))
         for k in wr:
-            wr_[k], rd_[k] = [tok], []
+            if not is_bank(k):
+                before.update(wr_.get(k, []) + rd_.get(k, []))
+        for k in rd:
+            rd_.setdefault(k, []).append(n)
+        for k in wr:
+            wr_[k], rd_[k] = [n], []
+        before.discard(n)
+        rec.append((e, sem, inc, before, order, cost, late, call))
+        return n
 
     def op(e, rd, wr, name, *a, **kw):
-        toks = deps(e, rd, wr)
-        if e == "t":
-            toks = [x for x in toks if x[0] != "st"]
-        sync(e, toks)
         f = {"cp": lambda: g.vector.tensor_copy, "tt": lambda: g.vector.tensor_tensor, "ts": lambda: g.vector.tensor_scalar,
              "scan": lambda: g.vector.tensor_tensor_scan, "ms": lambda: g.vector.memset, "act": lambda: g.scalar.activation,
              "mm": lambda: g.tensor.matmul, "iota": lambda: g.iota}[name]()
-        s = SN[e]
-        cnt[s] += 1
-        f(*a, **kw).then_inc(S[s], 1)
-        snap[(s, cnt[s])] = dict(known[e])
-        note(e, (s, cnt[s]), rd, wr)
+        key = wr[0].rstrip("0123456789")
+        c = (0.3 if wr[0] in ("b5", "b6") else 0.045) if e == "t" else US[e].get(key, 0.11) if e in US else 0.3
+        add(e, SN[e], 1, rd, wr, c, 0.0, lambda: f(*a, **kw))
 
     def dma(e, sem, out, in_, rd, wr):
-        sync(e, deps(e, rd, wr))
-        cnt[sem] += 16
-        Q[e].dma_start(out, in_).then_inc(S[sem], 16)
-        snap[(sem, cnt[sem])] = dict(known[e])
-        note(e, (sem, cnt[sem]), rd, wr)
+        return add(e, sem, 16, rd, wr, 0.1, LOADED.get(sem, 2.5), lambda: Q[e].dma_start(out, in_))
+
+    def issue():
+        todo = {e: [i for i in range(len(rec)) if rec[i][0] == e] for e in Q}
+        now, fin = {e: 0.0 for e in Q}, {}
+        for i in range(len(rec)):
+            if rec[i][0] is None:
+                fin[i] = None
+        left, pos = sum(len(x) for x in todo.values()), {}
+        while left:
+            best = None
+            for e in Q:
+                head = pick = None
+                for i in todo[e][:WINDOW[e]]:
+                    st = now[e]
+                    for d in rec[i][3] | rec[i][4]:
+                        f = fin.get(d)
+                        if rec[d][0] is None:
+                            f = fin.get(rec[d][3])
+                            f = None if f is None else f + 2.0
+                        if f is None:
+                            st = None
+                            break
+                        if d in rec[i][3] and f > now[e] - WAKE:
+                            st = max(st, f + WAKE)
+                    if head is None:
+                        head = (st, i)
+                        if st is not None:
+                            pick = (st, i)
+                    elif st is not None and (pick is None or (st < pick[0] and (head[0] is None or st + rec[i][5] <= head[0] + 0.04))):
+                        pick = (st, i)
+                if pick is not None and (best is None or pick[0] < best[0]):
+                    best = (pick[0], e, pick[1])
+            st, e, i = best
+            _, sem, inc, before, order, cost, late, call = rec[i]
+            todo[e].remove(i)
+            left -= 1
+            now[e] = st + cost
+            fin[i] = st + cost + late
+            toks = []
+            for d in before:
+                if not (e == "t" and rec[d][0] == "t"):
+                    toks.append(pos[d] if rec[d][0] is not None else (rec[d][1], rec[d][2]))
+            sync(e, toks)
+            cnt[sem] += inc
+            pos[i] = (sem, cnt[sem])
+            ins = call()
+            if sem != "loc":
+                ins.then_inc(S[sem], inc)
+            snap[pos[i]] = dict(known[e])
 
     def V(rd, wr, name, *a):
         op("v", rd, wr, name, *a)
@@ -134,12 +188,15 @@ def rank_program(g, core, T, topo):
     def blk(name, r):
         return T[name][:, 128 * r:128 * (r + 1)]
 
-    def land(key, sem, n=12):
-        cnt[sem] += n
-        wr_[key] = [(sem, cnt[sem])]
+    lands = {}
+
+    def land(key, sem):
+        cnt[sem] += 12
+        lands[sem] = len(rec)
+        wr_[key] = [len(rec)]
+        rec.append((None, sem, 12, None, set(), 0.0, 0.0, None))
 
     def send(sem, pieces, rd):
-        sync("g", deps("g", rd, []))
         tr = []
         for n, p in enumerate(peers):
             rid, pid, _ = topo.addr(T.cores[p])
@@ -147,10 +204,8 @@ def rank_program(g, core, T, topo):
             eng = topo.engines(core, T.cores[p])
             tr.append(RemoteDMATransfer(dst_ids=[DstId(rid=rid, pnc=pid)], dma_engine_mask=sum(1 << x for x in eng[4 * n:4 * n + 4]),
                                         remote_sem=S[sem], src=src, dst=dst))
-        g.remote_dma_fused(tr, local_sem=S.loc)
-        cnt["loc"] += 12
-        snap[("loc", cnt["loc"])] = dict(known["g"])
-        note("g", ("loc", cnt["loc"]), rd, [])
+        n = add("g", "loc", 12, rd, [], 0.3, 1.0, lambda: g.remote_dma_fused(tr, local_sem=S.loc))
+        rec[lands[sem]] = (None, sem, 12, n, set(), 0.0, 0.0, None)
 
     for t in range(4):
         land("SM%dp" % t, "pre%d" % t)
@@ -160,14 +215,24 @@ def rank_program(g, core, T, topo):
         land("LT%dr" % t, "ft%d" % t)
     dma("y", "dwk", T.WKI[:], T.wk[:], [], ["WKI"])
     dma("s", "dfm", T.M[:, 0:256], T.fm[:], [], ["M0"])
-    dma("s", "dlm", T.TAB[:, 4096:6144], T.lm[:], [], ["LM"])
-    dma("y", "dfr", T.FR[:], T.fr[:], [], ["FR"])
+    dma("y", "dlm", T.TAB[:, 4096:6144], T.lm[:], [], ["LM"])
     dma("y", "dtl", T.TLI[:], T.tl[:], [], ["TLI"])
-    dma("s", "dmo", T.MO[:], T.mo[:], [], ["MO"])
+    dma("y", "dmo", T.MO[:], T.mo[:], [], ["MO"])
+    dma("y", "dfr", T.FR[:], T.fr[:], [], ["FR"])
     dma("y", "dsn", T.TAB[:, 0:4096], T.sn[:], [], ["SN"])
+    rf = []
+    for t in range(4):
+        rf.append(dma("y", "drf", T["SM%d" % t][:, 256 * rank:256 * rank + 48], T.fr[:, 256 * t + 48 * rank:256 * t + 48 * rank + 48], [], ["SM%do" % t]))
+        rf.append(dma("y", "drf", T.M[:, 256 * t + 448:256 * t + 512], T.fr[:, 256 * t + 192:256 * t + 256], [], ["M%df" % (t + 1)]))
+    for t in range(4):
+        wr_["SM%do" % t], wr_["M%df" % (t + 1)] = list(rf), list(rf)
 
     op("g", [], ["CI"], "iota", T.CI[:], [[1, 256]], 0, 0)
     op("g", [], ["PI"], "iota", T.PI[:], [[0, 1]], 0, 1)
+    for t in range(3):
+        for d in range(4):
+            op("g", [], ["ST%d_%d" % (t, d)], "iota", T["ST%d" % t][:, 256 * d:256 * d + 48], [[0, 48]], 0, 0, allow_small_or_imprecise_dtypes=True)
+        op("g", [], ["LT%df" % (t + 1)], "iota", T.LT[:, 256 * t + 192:256 * t + 256], [[0, 64]], 0, 0, allow_small_or_imprecise_dtypes=True)
     for t in range(4):
         send("pre%d" % t, lambda p: (T["SM%d" % t][:, 256 * rank:256 * rank + 48], T.FR[:, 256 * t + 48 * p:256 * t + 48 * p + 48]), ["FR"])
     rp, gp, pf = T.PF[:, 0:1], T.PF[:, 1:2], T.PF[:, 2:3]
@@ -242,20 +307,20 @@ def rank_program(g, core, T, topo):
         for t in range(3):
             V(["FR"], ["MREF%d" % t], "cp", T.MREF[:, 64 * t:64 * t + 64], T.FR[:, 256 * t + 192:256 * t + 256])
 
-    def constants_s():
-        for t in range(4):
-            SA(["FR"], ["M%df" % (t + 1)], T.M[:, 256 * t + 448:256 * t + 512], T.FR[:, 256 * t + 192:256 * t + 256])
-            SA(["FR"], ["SM%do" % t], T["SM%d" % t][:, 256 * rank:256 * rank + 48], T.FR[:, 256 * t + 48 * rank:256 * t + 48 * rank + 48])
-        for t in range(3):
-            SA(["ZER"], ["LT%df" % (t + 1)], T.LT[:, 256 * t + 192:256 * t + 256], T.ZER[:, 0:64])
-            for d in range(4):
-                SA(["ZER"], ["ST%d_%d" % (t, d)], T["ST%d" % t][:, 256 * d:256 * d + 48], T.ZER[:, 0:48])
-        for r in range(16):
-            SA(["BLK", "ROW"], ["SEL%d" % r], blk("SEL", r), T.BLK[:], scale=T.ROW[:, r:r + 1])
-        for r in range(16):
-            SA(["MS%d" % r, "TRC"], ["TRI%d" % r], blk("TRI", r), blk("MS", r), scale=T.TRC[:, r:r + 1])
-        mm(["SEL0", "KB"], "b2", T.b2[:, 0:1], blk("SEL", 0), T.KB[:, 1:2], True, True)
-        V(["b2"], ["K0"], "cp", T.K0[:], T.b2[:, 0:1])
+    def constants_s(part):
+        if part == 0:
+            SA(["BLK", "ROW"], ["SEL0"], blk("SEL", 0), T.BLK[:], scale=T.ROW[:, 0:1])
+            mm(["SEL0", "KB"], "b7", T.b7[:, 200:201], blk("SEL", 0), T.KB[:, 1:2], True, True)
+        if part == 1:
+            for r in range(1, 16):
+                SA(["BLK", "ROW"], ["SEL%d" % r], blk("SEL", r), T.BLK[:], scale=T.ROW[:, r:r + 1])
+        if part == 2:
+            for i in range(16):
+                SA(MRK, ["MXR%d" % i], T.MXR[:, i::16], T.MREF[:])
+            wr_["MXR"] = [n for i in range(16) for n in wr_["MXR%d" % i]]
+        if part == 3:
+            for r in range(16):
+                SA(["MS%d" % r, "TRC"], ["TRI%d" % r], blk("TRI", r), blk("MS", r), scale=T.TRC[:, r:r + 1])
     C256K = ["C256_%d" % d for d in range(4)]
     MRK = ["MREF0", "MREF1", "MREF2"]
 
@@ -270,11 +335,12 @@ def rank_program(g, core, T, topo):
                 ta += a[0][0]
                 a.pop(0)[1]()
 
-    def pipe(chunks, gather, diff, post, after):
+    def pipe(chunks, gather, diff, post, after, ahead=0):
         out, n = [], len(chunks)
 
         def g1(k):
-            gather(chunks[k])
+            if k >= ahead:
+                gather(chunks[k])
             diff(chunks[k], "b%d" % (5 + k % 2))
 
         def p1(k):
@@ -288,19 +354,55 @@ def rank_program(g, core, T, topo):
         return out
 
     def share(sc):
-        vp = [(c, c + 2) for c in range(0, 16, 2) if (c, c + 2) not in sc]
-        ends, k = {}, 0
-        while k < len(vp):
-            j = k + 1 if k + 1 < len(vp) and vp[k + 1][0] == vp[k][1] else k
-            ends[vp[j][1] - 1] = vp[k][0]
-            k = j + 1
-        return vp, ends
+        return [(c, c + 2) for c in range(0, 16, 2) if (c, c + 2) not in sc]
 
-    def sums(bank, sel, c0, c1, state):
-        state[0] += c1 - c0
+    def sums(bank, sel, c0, c1, done):
+        done.update(range(c0, c1))
+        k = c0 // 4 * 4
+        if not all(c in done for c in range(k, k + 4)):
+            return
         for r in range(16):
-            mm(["FL%d" % c for c in range(c0, c1)] + ([sel] if sel == "VN" else ["MS%d" % r]), bank, T[bank][:, 16 * c0:16 * c1], blk(sel, r),
-               T.FL[:, c0:c1, 16 * r:16 * r + 16], False, bool(state[0] == 16 and r == 15))
+            mm(["FL%d" % c for c in range(k, k + 4)] + ([sel] if sel == "VN" else ["MS%d" % r]), bank, T[bank][:, 16 * k:16 * k + 64], blk(sel, r),
+               T.FL[:, k:k + 4, 16 * r:16 * r + 16], False, bool(len(done) == 16 and r == 15))
+
+    def spread_keys():
+        V(["KEY"], ["KPa"], "ts", T.KP[:, 0:16], P["KEY"], 8160, None, A.bitwise_and)
+        V(["KEY"], ["KPb"], "ts", T.KP[:, 16:32], P["KEY"], 31, None, A.bitwise_and)
+        V(["KPa", "KPb"], ["KPB"], "cp", T.KPB[:], T.KP[:])
+        V(["KEY"], ["NKF"], "ts", T.NKF[:], P["KEY"], -1.0, None, A.mult)
+        for r in range(16):
+            mm(["SEL%d" % r, "KPB"], "b3", T.b3[:, r:256:16], blk("SEL", r), T.KPB[:, 0:16], True, False)
+            mm(["SEL%d" % r, "KPB"], "b3", T.b3[:, r:256:16], blk("SEL", r), T.KPB[:, 16:32], False, True)
+        ops(("cp", "KF", "KEY"))
+
+    def equal_pairs(first_s):
+        V(["b3"], ["KR"], "cp", T.KR[:], T.b3[:, 0:256])
+        off = 0
+        for c in range(first_s, 16):
+            n = 256 - 16 * c
+            SA(["b3", "NKF"], ["EQT%d" % c], T.EQT[:, off:off + n], T.b3[:, 16 * c:256], F.Abs, bias=T.NKF[:, c:c + 1])
+            SA(["EQT%d" % c], ["EQ%d" % c], T.EQ[:, 272 * c:256 * c + 256], T.EQT[:, off:off + n], F.Relu, bias=1.0, scale=-1.0)
+            off += n
+        mm(["IDN", "ZER"], "b4", T.b4[:, 0:256], T.IDN[:], T.ZER[:], True, False)
+        for c in range(16):
+            if c < first_s:
+                V(["KR", "KF"], ["EQ%d" % c], "ts", T.EQ[:, 272 * c:256 * c + 256], T.KR[:, 16 * c:256], T.KF[:, c:c + 1], None, A.is_equal)
+            if c < 15:
+                mm(["BLK", "EQ%d" % c], "b4", T.b4[:, 16 * c + 16:256], T.BLK[:], T.EQ[:, 272 * c + 16:256 * c + 256], False, c == 14)
+
+    def earlier_lanes():
+        SA(["b4"], ["DUPS"], T.DUPS[:], T.b4[:, 0:256])
+
+    def count_earlier():
+        for r in range(16):
+            mm(["TRI%d" % r] + ["EQ%d" % c for c in range(16)], "b7", T.b7[:, 128:144], blk("TRI", r), T.EQ[:, r::272], r == 0, False)
+        for r in range(16):
+            mm(["MS%d" % r, "DUPS"], "b7", T.b7[:, 128:144], blk("MS", r), T.DUPS[:, r::16], False, r == 15)
+
+    def winners():
+        V(["KF", "L6"], ["A1"], "tt", P["A1"], T.KF[:], P["L6"], A.subtract)
+        V(["b7"], ["WIN"], "ts", P["WIN"], T.b7[:, 128:144], 0.0, None, A.is_equal)
+        ops(("tt", "A2", "A1", "WIN", A.mult))
 
     LM, SNW = T.TAB[:, 4096:6144], T.TAB[:, 0:4096]
     MXK, ZXK = ["MX%d" % i for i in range(16)], ["ZX%d" % i for i in range(16)]
@@ -333,18 +435,9 @@ def rank_program(g, core, T, topo):
                 SA([b], ["FL%d" % c], T.FL[:, c, :], T[b][:, o:o + 256], F.Relu)
         mm(["BLK", "RHK"], "b3", T.b3[:, 0:256], T.BLK[:], T.RHK[:], True, False)
         mm(["IDN", "JC"], "b3", T.b3[:, 0:256], T.IDN[:], T.JC[:], False, False)
-        lst8 = [0]
-        vp, ends = share(LS)
+        lst8 = set()
+        vp = share(LS)
         st = pipe(LS, lgather, ldiff, lpost, lambda ch: sums("b3", "VN", ch[0], ch[1], lst8))
-        if t:
-            candidates(192, T.M[:, 256 * t:256 * t + 192], mk[:2], T.LST[:, 0:192], "LST", T.AR[:, 0:192], "AR")
-            for k in range(3):
-                st.pop(0)[1]()
-            for i in range(16):
-                if i >= MX_V:
-                    SA(mk[:2], ["MX%d" % i], T.MX[:, i:3072:16], T.M[:, 256 * t:256 * t + 192])
-            for i in range(MX_V):
-                V(mk[:2], ["MX%d" % i], "cp", T.MX[:, i:3072:16], T.M[:, 256 * t:256 * t + 192])
         for k, w in ((0, "WU"), (16, "WV")):
             for r in range(16):
                 mm([w] + mk, "b2", T.b2[:, k:k + 16], blk(w, r), T.M[:, 256 * t + r:256 * t + 256:16], r == 0, r == 15)
@@ -353,9 +446,8 @@ def rank_program(g, core, T, topo):
             def lv(c=c):
                 o, mx, k1, k2 = lsrc(c, c + 1)
                 V(["LM"] + k1 + k2, ["FL%d" % c], "tt", T.FL[:, c, :], LM.indirect(o), mx, A.is_gt)
-                if c in ends:
-                    sums("b3", "VN", ends[c], c + 1, lst8)
-            vt.append((EST["vL"], lv))
+                sums("b3", "VN", c, c + 1, lst8)
+            vt.append((EST["vL"] + (1.0 if t and not vt else 0.0), lv))
         merge(vt, st)
         V(["b2"], ["TUI"], "ts", T.TUI[:], T.b2[:, 0:32], -1.0, None, A.mult)
         ops(("ts", "TUI", "TUI", 4095, None, A.bitwise_and))
@@ -363,7 +455,6 @@ def rank_program(g, core, T, topo):
         ops(("ts", "TAL", "TPR", 5, 2047, A.arith_shift_right, A.bitwise_and))
         if t == 0:
             constants_2()
-            candidates(192, T.MREF[:], MRK, T.LSTR[:], "LSTR", T.ARF[:], "ARF")
             SA(["SN"], ["SN"], T.TAB[:, 0:4096], T.TAB[:, 0:4096], F.Identity, bias=255.0, scale=-1.0)
         V(["SEG", "b3"], ["SC"], "scan", T.SC[:], T.SEG[:], T.b3[:, 0:256], 0.0, A.mult, A.max)
         V(["SC"], ["KK"], "cp", P["KK"], T.SC[:, 15::16])
@@ -373,6 +464,17 @@ def rank_program(g, core, T, topo):
         V(["TL", "GL"], ["TG"], "cp", T.TG[:], T.TL[:, 0:2048].indirect(P["GL"]))
         V(["LM", "GL", "MN"], ["ZQ"], "tt", T.ZQ[:], LM.indirect(P["GL"]), T.MN[:], A.add)
         SA(mk, ["Rm"], T.R[:, 4096:4352], m)
+        if t == 3:
+            V(["TUI", "K0"], ["C0T"], "ts", P["C0T"], T.TUI[:, 0:16], T.K0[:], None, A.mult)
+            V(["SC"], ["NOH"], "ts", P["NOH"], T.SC[:, 15::16], 128.0, None, A.is_lt)
+            ops(("tt", "C0T", "C0T", "TAL", A.add), ("ts", "C0I", "C0T", 2047, None, A.bitwise_and), ("tt", "A1", "C0I", "L2", A.subtract),
+                ("tt", "A2", "A1", "NOH", A.mult), ("tt", "KEY", "A2", "L6", A.add))
+            spread_keys()
+
+        def pgather(ch):
+            SA(["MO", "TG"], ["X%d" % ch[0]], T.X[:, 256 * ch[0]:256 * ch[1]], T.MO[:].indirect(T.TG[:, 16 * ch[0]:16 * ch[1]]))
+        pgather(P_S[0])
+        pgather(P_S[1])
         for i in range(16):
             if i < ZX_S:
                 SA(["ZQ"], ["ZX%d" % i], T.ZX[:, i::16], T.ZQ[:])
@@ -382,12 +484,15 @@ def rank_program(g, core, T, topo):
             mm(["IDN", "ZER"], b, T[b][:, 0:256], T.IDN[:], T.ZER[:], True, False)
             mm(["WBU", "C255"], b, T[b][:, 0:128], T.WBU[:], T.C255[:, 0:128], False, False)
             mm(["WBV", "C255"], b, T[b][:, 128:256], T.WBV[:], T.C255[:, 0:128], False, False)
+        if t == 3:
+            equal_pairs(16)
         nh, done = [0, 0], {}
 
         def hsum(ch):
-            done[ch[0]] = True
+            for c in range(*ch):
+                done[c] = True
             k = ch[0] // 4 * 4
-            if not (k in done and k + 2 in done):
+            if not all(c in done for c in range(k, k + 4)):
                 return
             c0, c1, h = k, k + 4, k // 8
             b, l0, n = "b%d" % h, 16 * c0 - 128 * h, 64
@@ -397,9 +502,6 @@ def rank_program(g, core, T, topo):
                     mm(["R%d" % c for c in range(c0, c1)] + [w], b, T[b][:, o + l0:o + l0 + n], blk(w, i),
                        T.R[:, 256 * c0 + i:256 * c1:16], False, bool(nh[h] == 8 and o and i == 15))
 
-        def pgather(ch):
-            SA(["MO", "TG"], ["X%d" % ch[0]], T.X[:, 256 * ch[0]:256 * ch[1]], T.MO[:].indirect(T.TG[:, 16 * ch[0]:16 * ch[1]]))
-
         def pdiff(ch, b):
             mm(["IDN", "X%d" % ch[0]], b, T[b][:], T.IDN[:], T.X[:, 256 * ch[0]:256 * ch[1]], True, False)
             mm(["IDM"] + ZXK, b, T[b][:], T.IDM[:], T.ZX[:, 256 * ch[0]:256 * ch[1]], False, True)
@@ -407,7 +509,7 @@ def rank_program(g, core, T, topo):
         def ppost(ch, b):
             SA([b], ["R%d" % c for c in range(*ch)], T.R[:, 256 * ch[0]:256 * ch[1]], T[b][:], F.Relu, scale=-1.0)
         vt = []
-        for ch in share(P_S)[0]:
+        for ch in P_V:
             def pv1(ch=ch):
                 c0, c1 = ch
                 V(["MO", "TG"] + ZXK, ["TT%d" % c0], "tt", T.TT[:, 256 * c0:256 * c1], T.MO[:].indirect(T.TG[:, 16 * c0:16 * c1]),
@@ -417,15 +519,19 @@ def rank_program(g, core, T, topo):
                 c0, c1 = ch
                 V(["TT%d" % c0], ["R%d" % c for c in range(c0, c1)], "ts", T.R[:, 256 * c0:256 * c1], T.TT[:, 256 * c0:256 * c1], -1.0, 0.0, A.mult, A.max)
                 hsum(ch)
-            vt += [(EST["vT"], pv1), (EST["vR"], pv2)]
-        vt[0] = (EST["vT"] + 0.1 * (16 - ZX_S), vt[0][1])
-        st = pipe(P_S, pgather, pdiff, ppost, hsum)
+            n = (ch[1] - ch[0]) / 2
+            vt += [(EST["vT"] * n, pv1), (EST["vR"] * n, pv2)]
+        st = pipe(P_S, pgather, pdiff, ppost, hsum, 2)
+        st[0] = (0.2, st[0][1])
+        st[1] = (0.2, st[1][1])
         if t == 0:
-            for i in range(16):
-                SA(MRK, ["MXR%d" % i], T.MXR[:, i::16], T.MREF[:])
-            wr_["MXR"] = wr_["MXR15"]
-            constants_s()
+            constants_s(0)
         merge(vt, st)
+        if t == 3:
+            earlier_lanes()
+            count_earlier()
+        if t == 0:
+            constants_s(1)
         if t < 3:
             SA(["TL", "GL"], ["TGF"], T.TGF[:], T.TL[:, 0:2048].indirect(P["GL"]), F.Identity, bias=8192.0)
             SA(["TL", "NBC0", "NBC1"], ["NB"], T.NB[:], T.TL[:, 0:256], F.Identity, bias=T.NBC[:, 1:2], scale=T.NBC[:, 0:1])
@@ -442,7 +548,7 @@ def rank_program(g, core, T, topo):
             V(["HI"], ["HL%d" % h], "cp", T.HL[:, o], T.HI[:, o])
         hashes(0)
         mm(["IDN", "ZER"], "b4", T.b4[:, 0:256], T.IDN[:], T.ZER[:], True, False)
-        sst = [0]
+        sst = set()
 
         def sgather(ch):
             SA(["SN", "HL%d" % (ch[0] // 8)], ["X%d" % ch[0]], T.X[:, 256 * ch[0]:256 * ch[1]], SNW.indirect(T.HL[:, 16 * ch[0]:16 * ch[1]]))
@@ -455,14 +561,12 @@ def rank_program(g, core, T, topo):
             for c in range(ch[0], ch[1]):
                 o = 256 * (c - ch[0])
                 SA([b], ["FL%d" % c], T.FL[:, c, :], T[b][:, o:o + 256], F.Square)
-        vp, ends = share(S_S)
         vt = []
-        for c in [c for p in vp for c in range(*p)]:
-            def sv(c=c, ends=ends):
+        for c in [c for p in share(S_S) for c in range(*p)]:
+            def sv(c=c):
                 V(["SN", "HL%d" % (c // 8), "R%d" % c], ["FL%d" % c], "tt", T.FL[:, c, :], SNW.indirect(T.HL[:, 16 * c:16 * c + 16]),
                   T.R[:, 256 * c:256 * c + 256], A.not_equal)
-                if c in ends:
-                    sums("b4", "MS", ends[c], c + 1, sst)
+                sums("b4", "MS", c, c + 1, sst)
             vt.append((EST["vL"], sv))
         vt.insert(2, (1.3, lambda: hashes(1)))
         merge(vt, pipe(S_S, sgather, sdiff, spost, lambda ch: sums("b4", "MS", ch[0], ch[1], sst)))
@@ -476,8 +580,13 @@ def rank_program(g, core, T, topo):
         for k, w in ((0, "WU"), (16, "WV")):
             for r in range(16):
                 mm([w, "PCB"], "b2", T.b2[:, k:k + 16], blk(w, r), T.PCB[:, r::16], r == 0, r == 15)
-        ops(("cp", "LSEL", "VH"))
+        if t == 3:
+            winners()
+            ops(("tt", "A3", "A2", "L2", A.add), ("cp", "LLb", "A3"))
+            V(["LLb"] + mk, ["LM"], "cp", T.TAB[:, 4096:6400].indirect(P["LLb"]), m)
+            dma("y", "dyl", T.yl[:], T.TAB[:, 4096:6144], ["LM"], [])
         if t < 3:
+            ops(("cp", "LSEL", "VH"))
             src = T.NB
             sk = ["NB"]
             if t:
@@ -489,13 +598,18 @@ def rank_program(g, core, T, topo):
             SA(["MT1"], ["MK"], T.MK[:], T.MT1[:], F.Relu, bias=1.0, scale=-1.0)
             SA(["MT1"], ["MT1"], T.MT1[:], T.MT1[:], F.Abs, bias=-2048.0)
             SA(["MT1"], ["MT2"], T.MT2[:], T.MT1[:], F.Identity, bias=2048.0, scale=-1.0)
-        ops(("ts", "NONE", "VH", 0.0, None, A.is_equal), ("ts", "CH", "VH", 0.0, None, A.is_gt), ("ts", "N8", "VH", 0.0, 8.0, A.is_equal, A.mult),
-            ("tt", "NN", "NONE", "L1", A.mult), ("tt", "A3", "NONE", "L6", A.mult))
-        V(["TUI", "K0"], ["C0T"], "ts", P["C0T"], T.TUI[:, 0:16], T.K0[:], None, A.mult)
-        ops(("tt", "NA", "NOH", "BD", A.mult), ("tt", "C0T", "C0T", "TAL", A.add), ("tt", "PLB", "NA", "PLF", A.add),
-            ("ts", "C0I", "C0T", 2047, None, A.bitwise_and), ("cp", "PL2", "PLB"), ("tt", "A1", "C0I", "L2", A.subtract),
-            ("tt", "A2", "A1", "NOH", A.mult), ("tt", "KA", "A2", "A3", A.add))
-        SA(["PL2"] + RK, ["VAL"], T.VAL[:], T.R[:].indirect(P["PL2"]))
+        ops(("ts", "NONE", "VH", 0.0, None, A.is_equal), ("ts", "N8", "VH", 0.0, 8.0, A.is_equal, A.mult), ("tt", "NN", "NONE", "L1", A.mult))
+        if t == 0:
+            V(["b7"], ["K0"], "cp", T.K0[:], T.b7[:, 200:201])
+        if t < 3:
+            V(["TUI", "K0"], ["C0T"], "ts", P["C0T"], T.TUI[:, 0:16], T.K0[:], None, A.mult)
+            ops(("tt", "NA", "NOH", "BD", A.mult), ("tt", "C0T", "C0T", "TAL", A.add), ("tt", "PLB", "NA", "PLF", A.add),
+                ("ts", "C0I", "C0T", 2047, None, A.bitwise_and), ("cp", "PL2", "PLB"), ("tt", "A1", "C0I", "L2", A.subtract),
+                ("ts", "CH", "VH", 0.0, None, A.is_gt), ("tt", "A3", "NONE", "L6", A.mult), ("tt", "A2", "A1", "NOH", A.mult), ("tt", "KA", "A2", "A3", A.add))
+            SA(["PL2"] + RK, ["VAL"], T.VAL[:], T.R[:].indirect(P["PL2"]))
+        if t == 0:
+            candidates(192, T.MREF[:], MRK, T.LSTR[:], "LSTR", T.ARF[:], "ARF")
+            constants_s(2)
         V(["b2"], ["CUI"], "ts", T.CUI[:], T.b2[:, 0:32], -1.0, None, A.mult)
         ops(("ts", "CUI", "CUI", 4095, None, A.bitwise_and))
         V(["CUI"], ["CPR"], "tt", P["CPR"], T.CUI[:, 0:16], T.CUI[:, 16:32], A.mult)
@@ -509,7 +623,8 @@ def rank_program(g, core, T, topo):
         mm(["NTR"] + EK, "b7", T.b7[:, 64:128], T.NTR[:], T.E[:], False, False)
         V(["SEG"] + EK, ["CS"], "scan", T.CS[:], T.SEG[:, 0:64], T.E[:], 0.0, A.mult, A.add)
         mm(["BLK", "CS"], "b7", T.b7[:, 64:128], T.BLK[:], T.CS[:], False, True)
-        ops(("ts", "CHH", "CPS", 4095, None, A.bitwise_and), ("tt", "KH", "CHH", "CH", A.mult), ("tt", "KEY", "KH", "KA", A.add))
+        if t < 3:
+            ops(("ts", "CHH", "CPS", 4095, None, A.bitwise_and), ("tt", "KH", "CHH", "CH", A.mult), ("tt", "KEY", "KH", "KA", A.add))
         V(["b7"] + EK, ["SL"], "tt", T.SL[:], T.b7[:, 64:128], T.E[:], A.mult)
         V(["SL"], ["S2"], "tt", T.S2[:], T.SL[:, 0:32], T.SL[:, 32:64], A.add)
         V(["S2"], ["S3"], "tt", P["S3"], T.S2[:, 0:16], T.S2[:, 16:32], A.add)
@@ -518,54 +633,35 @@ def rank_program(g, core, T, topo):
         V(["SLOT", "PCB", "SM%dp" % t, "SM%do" % t], ["SM%d" % t], "cp", sm[:].indirect(P["SLOT"]), T.PCB[:])
         send("fm%d" % (t + 1), lambda p: (T.M[:, nx + 48 * rank:nx + 48 * rank + 48], sm[:, 256 * p:256 * p + 48]), ["SM%d" % t])
         SA(["SM%d" % t], ["M%do" % (t + 1)], T.M[:, nx + 48 * rank:nx + 48 * rank + 48], sm[:, 256 * rank:256 * rank + 48])
-        V(["KEY"], ["KPa"], "ts", T.KP[:, 0:16], P["KEY"], 8160, None, A.bitwise_and)
-        V(["KEY"], ["KPb"], "ts", T.KP[:, 16:32], P["KEY"], 31, None, A.bitwise_and)
-        V(["KPa", "KPb"], ["KPB"], "cp", T.KPB[:], T.KP[:])
-        V(["KEY"], ["NKF"], "ts", T.NKF[:], P["KEY"], -1.0, None, A.mult)
-        for r in range(16):
-            mm(["SEL%d" % r, "KPB"], "b3", T.b3[:, r:256:16], blk("SEL", r), T.KPB[:, 0:16], True, False)
-            mm(["SEL%d" % r, "KPB"], "b3", T.b3[:, r:256:16], blk("SEL", r), T.KPB[:, 16:32], False, True)
-        ops(("cp", "KF", "KEY"))
+        if t == 0:
+            constants_s(3)
         if t < 3:
+            spread_keys()
             stt = T["ST%d" % t]
             V(["SLOT", "SELG", "TGF"] + ["ST%d_%d" % (t, d) for d in range(4)], ["ST%d" % t], "tt", stt[:].indirect(P["SLOT"]), T.SELG[:], T.TGF[:], A.max)
             send("ft%d" % (t + 1), lambda p: (T.LT[:, 256 * t + 48 * rank:256 * t + 48 * rank + 48], stt[:, 256 * p:256 * p + 48]), ["ST%d" % t])
-        V(["b3"], ["KR"], "cp", T.KR[:], T.b3[:, 0:256])
-        off = 0
-        for c in range(EQ_S, 16):
-            n = 256 - 16 * c
-            SA(["b3", "NKF"], ["EQT%d" % c], T.EQT[:, off:off + n], T.b3[:, 16 * c:256], F.Abs, bias=T.NKF[:, c:c + 1])
-            SA(["EQT%d" % c], ["EQ%d" % c], T.EQ[:, 272 * c:256 * c + 256], T.EQT[:, off:off + n], F.Relu, bias=1.0, scale=-1.0)
-            off += n
-        if t < 3:
+            equal_pairs(EQ_S)
             SA(["ST%d" % t], ["LT%do" % (t + 1)], T.LT[:, 256 * t + 48 * rank:256 * t + 48 * rank + 48], stt[:, 256 * rank:256 * rank + 48])
-        mm(["IDN", "ZER"], "b4", T.b4[:, 0:256], T.IDN[:], T.ZER[:], True, False)
-        for c in list(range(EQ_S)) + list(range(EQ_S, 16)):
-            if c < EQ_S:
-                V(["KR", "KF"], ["EQ%d" % c], "ts", T.EQ[:, 272 * c:256 * c + 256], T.KR[:, 16 * c:256], T.KF[:, c:c + 1], None, A.is_equal)
-            if c < 15:
-                mm(["BLK", "EQ%d" % c], "b4", T.b4[:, 16 * c + 16:256], T.BLK[:], T.EQ[:, 272 * c + 16:256 * c + 256], False, c == 14)
-        SA(["b4"], ["DUPS"], T.DUPS[:], T.b4[:, 0:256])
-        EQK = ["EQ%d" % c for c in range(16)]
+            earlier_lanes()
         if t == 0:
             V(["MK", "AR"], ["MKAa", "MKAb"], "tt", T.MKA[:], T.MK[:], T.AR[:], A.mult)
         elif t < 3:
             V(["MK", "AR"], ["MKAa"], "tt", T.MKA[:, 0:192], T.MK[:, 0:192], T.AR[:, 0:192], A.mult)
             V(["MK", "ARF"], ["MKAb"], "tt", T.MKA[:, 192:256], T.MK[:, 192:256], T.ARF[:, 64 * t - 64:64 * t], A.mult)
-        for r in range(16):
-            mm(["TRI%d" % r] + EQK, "b7", T.b7[:, 128:144], blk("TRI", r), T.EQ[:, r::272], r == 0, False)
-        for r in range(16):
-            mm(["MS%d" % r, "DUPS"], "b7", T.b7[:, 128:144], blk("MS", r), T.DUPS[:, r::16], False, r == 15)
-        V(["KF", "L6"], ["A1"], "tt", P["A1"], T.KF[:], P["L6"], A.subtract)
-        V(["b7"], ["WIN"], "ts", P["WIN"], T.b7[:, 128:144], 0.0, None, A.is_equal)
-        ops(("tt", "A2", "A1", "WIN", A.mult), ("tt", "A3", "A2", "L6", A.add), ("cp", "LLa", "A3"))
-        V(["LLa", "VAL"], ["LM", "SN"], "cp", T.TAB[:].indirect(P["LLa"]), T.VAL[:])
         if t < 3:
+            nk = ["M%dr" % (t + 1), "M%do" % (t + 1)]
+            candidates(192, T.M[:, nx:nx + 192], nk, T.LST[:, 0:192], "LST", T.AR[:, 0:192], "AR")
+            for i in range(16):
+                SA(nk, ["MX%d" % i], T.MX[:, i:3072:16], T.M[:, nx:nx + 192])
+            count_earlier()
+            winners()
+            ops(("tt", "A3", "A2", "L6", A.add), ("cp", "LLa", "A3"))
+            V(["LLa", "VAL"], ["LM", "SN"], "cp", T.TAB[:].indirect(P["LLa"]), T.VAL[:])
             ops(("tt", "A1", "A2", "NOH", A.mult), ("tt", "A3", "A1", "L2", A.add), ("cp", "LLb", "A3"))
             V(["LLb", "MT2", "MKAa", "MKAb"], ["TL"], "tt", T.TL[:].indirect(P["LLb"]), T.MT2[:], T.MKA[:], A.max)
-            V(["M%d%s" % (t + 1, x) for x in "rof"], ["MN"], "ts", T.MN[:], T.M[:, nx:nx + 256], -1.0, 255.0, A.mult, A.add)
-    dma("y", "dyl", T.yl[:], T.TAB[:, 4096:6144], ["LM"], [])
+            SA(["M%d%s" % (t + 1, x) for x in "rof"], ["MN"], T.MN[:], T.M[:, nx:nx + 256], F.Identity, bias=255.0, scale=-1.0)
     dma("s", "dyf", T.yf[:], T.M[:, 1024:1280], ["M4r", "M4o", "M4f"], [])
+    issue()
     for s in SEMAPHORES:
         if cnt[s] and known["y"].get(s, 0) < cnt[s]:
             g.sync.wait_ge(S[s], cnt[s])

from concourse.bass import DstId, RemoteDMATransfer
from concourse.mybir import AluOpType as A, ActivationFunctionType as F

BF, FP, I32, U16 = "bfloat16", "float32", "int32", "uint16"
POOLS = {
    "PLFP": ["LANE", "BASE", "BD", "L1", "L2", "L6", "HASF", "NOH", "VH", "PLF", "S3", "S4", "NN", "NONE", "N8", "CH", "A1", "A2",
             "A3", "KA", "KH", "WIN", "DD", "NA", "PLB"],
    "PLI": ["TPR", "TAL", "KK", "KC", "C0T", "C0I", "CPR", "CHH", "DI", "KEY", "CPS"],
    "PLU": ["GL", "LSEL", "PL", "SLOT", "PL2", "LLa", "LLb"],
}
SIZES = {
    BF: {"TAB": 6400, "MO": 2048, "FR": 1024, "M": 1280, "BLK": 128, "IDN": 128, "Z": 128, "NTR": 128, "ONES": 128, "DK": 128, "WBU": 128,
         "WBV": 128, "KUH": 128, "KUL": 128, "IDM": 128, "RHK": 256, "JC": 256, "KB": 2, "SEG": 256, "C255": 256, "ZER": 256, "C256": 64,
         "WU": 2048, "WV": 2048, "VN": 2048, "MS": 2048, "SEL": 2048, "TRI": 2048, "MREF": 192, "MX": 4096, "MXR": 3072, "X": 4096,
         "MN": 256, "ZQ": 256, "ZX": 4096, "R": 4352, "TT": 4096, "PCB": 256, "E": 64, "CS": 64, "KPB": 32, "EQ": 4096, "DUPS": 256,
         "VAL": 256, "SM0": 1280, "SM1": 1280, "SM2": 1280, "SM3": 1280},
    FP: {"TL": 2304, "PF": 4, "WF": 4, "WN": 4, "K0": 1, "CAP": 256, "TRC": 16, "ROW": 16, "SELM": 32, "NBC": 2, "COLF": 32, "SC": 256,
         "YY": 256, "SL": 64, "S2": 32, "TGF": 256, "SELG": 256, "LT": 768, "NB": 256, "MT": 256, "MK": 256, "MT1": 256, "MT2": 256,
         "MKA": 256, "KF": 16, "NKF": 16, "EQT": 1280, "ST0": 1280, "ST1": 1280, "ST2": 1280},
    I32: {"TLI": 2048, "WKI": 3, "CI": 256, "CM": 256, "PI": 1, "PR": 1, "PG": 1, "CG": 128, "KWI": 128, "KWT": 128, "UI": 512, "PRD": 256,
          "AR": 256, "ARF": 192, "CT": 256, "TUI": 32, "HP": 256, "HI": 256, "CUI": 32, "KP": 32},
    U16: {"LST": 256, "LSTR": 192, "TG": 256, "HL": 256, "KR": 256},
}
SCRATCH = {"FL": ("sbuf", [128, 16, 256], BF)}
for _d in SIZES:
    for _n in SIZES[_d]:
        SCRATCH[_n] = ("sbuf", [128, SIZES[_d][_n]], _d)
for _n, _d in (("PLFP", FP), ("PLI", I32), ("PLU", U16)):
    SCRATCH[_n] = ("sbuf", [128, 16 * len(POOLS[_n])], _d)
for _b in range(8):
    SCRATCH["b%d" % _b] = ("psum", [128, 512], FP)
_DMAS = ["wk", "fm", "fr", "lm", "tl", "mo", "sn", "rf", "yl", "yf"]
SEMAPHORES = (["sv", "ss", "st", "sg", "loc"] + ["d" + x for x in _DMAS]
              + ["pre%d" % t for t in range(4)] + ["fm%d" % t for t in range(1, 5)] + ["ft%d" % t for t in range(1, 4)])
L_S0 = [(12, 14), (14, 16), (8, 10)]
L_S = [(12, 14), (14, 16), (8, 10)]
P_S = [(4, 6), (6, 8), (12, 14), (14, 16)]
P_V = [(0, 4), (8, 12)]
S_S = [(4, 6), (6, 8), (14, 16)]
ZX_S, EQ_S = 4, 10
EST = {"vL": 0.47, "vT": 0.68, "vR": 0.26, "sG": 0.70, "sP": 0.53}

US = {"v": {"FL": 0.45, "TT": 1.35, "R": 0.48, "ZX": 0.16, "UI": 0.3, "PRD": 0.28, "AR": 0.2, "CT": 0.2, "LST": 0.2, "LSTR": 0.2, "SC": 0.26,
            "YY": 0.26, "TG": 0.42, "ZQ": 0.42, "SM": 0.9, "ST": 0.9, "LM": 0.9, "TL": 1.3, "MT": 0.45, "MKAa": 0.4, "KR": 0.26, "EQ": 0.12,
            "VN": 0.9, "ARF": 0.2, "HP": 0.15, "HI": 0.15, "HL": 0.15},
      "s": {"X": 0.72, "FL": 0.26, "R": 0.48, "MX": 0.21, "MXR": 0.21, "ZX": 0.26, "WU": 1.75, "WV": 1.75, "SN": 3.4, "TGF": 0.42, "NB": 0.26,
            "PCB": 0.42, "SELG": 0.42, "VAL": 0.42, "MT": 0.26, "MK": 0.26, "DUPS": 0.26, "MN": 0.26, "Rm": 0.26, "EQT": 0.13}}
LOADED = {"dlm": 6.0, "dtl": 10.0, "dmo": 13.0, "dfr": 14.0, "dsn": 18.0, "drf": 19.0}
WINDOW, WAKE = {"v": 60, "s": 4, "t": 60, "g": 1, "y": 1}, 0.1


def rank_program(g, core, T, topo):
    rank = T.rank_of(core)
    if rank is None:
        return
    peers = [r for r in range(len(T.cores)) if r != rank]
    S = T.sem
    Q = {"v": g.vector, "s": g.scalar, "t": g.tensor, "g": g, "y": g.sync}
    SN = {"v": "sv", "s": "ss", "t": "st", "g": "sg"}
    cnt = {k: 0 for k in SEMAPHORES}
    known = {e: {} for e in Q}
    snap, wr_, rd_, ps_ = {}, {}, {}, {}
    P = {}
    for pn in POOLS:
        for i, n in enumerate(POOLS[pn]):
            P[n] = T[pn][:, 16 * i:16 * i + 16]

    def is_bank(k):
        return k[0] == "b" and k[1:].isdigit()

    def sync(e, toks):
        need = {}
        for s, v in toks:
            if known[e].get(s, 0) < v:
                need[s] = max(need.get(s, 0), v)
        drop = [s for s in need if any(s2 != s and snap.get((s2, need[s2]), {}).get(s, 0) >= need[s] for s2 in need)]
        for s, v in need.items():
            if s not in drop:
                Q[e].wait_ge(S[s], v)
        for s, v in need.items():
            known[e][s] = max(known[e].get(s, 0), v)
            for a, b in snap.get((s, v), {}).items():
                known[e][a] = max(known[e].get(a, 0), b)

    rec = []

    def add(e, sem, inc, rd, wr, cost, late, call):
        n, before, order = len(rec), set(), set()
        for k in list(rd) + list(wr):
            if is_bank(k):
                cur = ps_.setdefault(k, [None, [], []])
                if cur[0] != e:
                    ps_[k] = cur = [e, [], cur[1]]
                before.update(cur[2])
                if e == "t":
                    order.update(cur[1][-1:])
                cur[1].append(n)
            elif k in rd:
                before.update(wr_.get(k, []))
        for k in wr:
            if not is_bank(k):
                before.update(wr_.get(k, []) + rd_.get(k, []))
        for k in rd:
            rd_.setdefault(k, []).append(n)
        for k in wr:
            wr_[k], rd_[k] = [n], []
        before.discard(n)
        rec.append((e, sem, inc, before, order, cost, late, call))
        return n

    def op(e, rd, wr, name, *a, **kw):
        f = {"cp": lambda: g.vector.tensor_copy, "tt": lambda: g.vector.tensor_tensor, "ts": lambda: g.vector.tensor_scalar,
             "scan": lambda: g.vector.tensor_tensor_scan, "ms": lambda: g.vector.memset, "act": lambda: g.scalar.activation,
             "mm": lambda: g.tensor.matmul, "iota": lambda: g.iota}[name]()
        key = wr[0].rstrip("0123456789")
        c = (0.3 if wr[0] in ("b5", "b6") else 0.045) if e == "t" else US[e].get(key, 0.11) if e in US else 0.3
        add(e, SN[e], 1, rd, wr, c, 0.0, lambda: f(*a, **kw))

    def dma(e, sem, out, in_, rd, wr):
        return add(e, sem, 16, rd, wr, 0.1, LOADED.get(sem, 2.5), lambda: Q[e].dma_start(out, in_))

    def issue():
        todo = {e: [i for i in range(len(rec)) if rec[i][0] == e] for e in Q}
        now, fin = {e: 0.0 for e in Q}, {}
        for i in range(len(rec)):
            if rec[i][0] is None:
                fin[i] = None
        left, pos = sum(len(x) for x in todo.values()), {}
        while left:
            best = None
            for e in Q:
                head = pick = None
                for i in todo[e][:WINDOW[e]]:
                    st = now[e]
                    for d in rec[i][3] | rec[i][4]:
                        f = fin.get(d)
                        if rec[d][0] is None:
                            f = fin.get(rec[d][3])
                            f = None if f is None else f + 2.0
                        if f is None:
                            st = None
                            break
                        if d in rec[i][3] and f > now[e] - WAKE:
                            st = max(st, f + WAKE)
                    if head is None:
                        head = (st, i)
                        if st is not None:
                            pick = (st, i)
                    elif st is not None and (pick is None or (st < pick[0] and (head[0] is None or st + rec[i][5] <= head[0] + 0.04))):
                        pick = (st, i)
                if pick is not None and (best is None or pick[0] < best[0]):
                    best = (pick[0], e, pick[1])
            st, e, i = best
            _, sem, inc, before, order, cost, late, call = rec[i]
            todo[e].remove(i)
            left -= 1
            now[e] = st + cost
            fin[i] = st + cost + late
            toks = []
            for d in before:
                if not (e == "t" and rec[d][0] == "t"):
                    toks.append(pos[d] if rec[d][0] is not None else (rec[d][1], rec[d][2]))
            sync(e, toks)
            cnt[sem] += inc
            pos[i] = (sem, cnt[sem])
            ins = call()
            if sem != "loc":
                ins.then_inc(S[sem], inc)
            snap[pos[i]] = dict(known[e])

    def V(rd, wr, name, *a):
        op("v", rd, wr, name, *a)

    def ops(*rows):
        for r in rows:
            name, out, ins = r[0], r[1], [x for x in r[2:] if isinstance(x, str)]
            V(ins, [out], name, *[ap(x) if isinstance(x, str) else x for x in r[1:]])

    def ap(n):
        return P[n] if n in P else T[n][:]

    def SA(rd, wr, out, in_, fn=F.Copy, **kw):
        op("s", rd, wr, "act", out, in_, fn, **kw)

    def mm(rd, bank, out, lhsT, rhs, start, stop):
        op("t", rd, [bank], "mm", out, lhsT, rhs, start, stop)

    def blk(name, r):
        return T[name][:, 128 * r:128 * (r + 1)]

    lands = {}

    def land(key, sem):
        cnt[sem] += 12
        lands[sem] = len(rec)
        wr_[key] = [len(rec)]
        rec.append((None, sem, 12, None, set(), 0.0, 0.0, None))

    def send(sem, pieces, rd):
        tr = []
        for n, p in enumerate(peers):
            rid, pid, _ = topo.addr(T.cores[p])
            dst, src = pieces(p)
            eng = topo.engines(core, T.cores[p])
            tr.append(RemoteDMATransfer(dst_ids=[DstId(rid=rid, pnc=pid)], dma_engine_mask=sum(1 << x for x in eng[4 * n:4 * n + 4]),
                                        remote_sem=S[sem], src=src, dst=dst))
        n = add("g", "loc", 12, rd, [], 0.3, 1.0, lambda: g.remote_dma_fused(tr, local_sem=S.loc))
        rec[lands[sem]] = (None, sem, 12, n, set(), 0.0, 0.0, None)

    for t in range(4):
        land("SM%dp" % t, "pre%d" % t)
    for t in range(1, 5):
        land("M%dr" % t, "fm%d" % t)
    for t in range(1, 4):
        land("LT%dr" % t, "ft%d" % t)
    dma("y", "dwk", T.WKI[:], T.wk[:], [], ["WKI"])
    dma("s", "dfm", T.M[:, 0:256], T.fm[:], [], ["M0"])
    dma("y", "dlm", T.TAB[:, 4096:6144], T.lm[:], [], ["LM"])
    dma("y", "dtl", T.TLI[:], T.tl[:], [], ["TLI"])
    dma("y", "dmo", T.MO[:], T.mo[:], [], ["MO"])
    dma("y", "dfr", T.FR[:], T.fr[:], [], ["FR"])
    dma("y", "dsn", T.TAB[:, 0:4096], T.sn[:], [], ["SN"])
    rf = []
    for t in range(4):
        rf.append(dma("y", "drf", T["SM%d" % t][:, 256 * rank:256 * rank + 48], T.fr[:, 256 * t + 48 * rank:256 * t + 48 * rank + 48], [], ["SM%do" % t]))
        rf.append(dma("y", "drf", T.M[:, 256 * t + 448:256 * t + 512], T.fr[:, 256 * t + 192:256 * t + 256], [], ["M%df" % (t + 1)]))
    for t in range(4):
        wr_["SM%do" % t], wr_["M%df" % (t + 1)] = list(rf), list(rf)

    op("g", [], ["CI"], "iota", T.CI[:], [[1, 256]], 0, 0)
    op("g", [], ["PI"], "iota", T.PI[:], [[0, 1]], 0, 1)
    for t in range(3):
        for d in range(4):
            op("g", [], ["ST%d_%d" % (t, d)], "iota", T["ST%d" % t][:, 256 * d:256 * d + 48], [[0, 48]], 0, 0, allow_small_or_imprecise_dtypes=True)
        op("g", [], ["LT%df" % (t + 1)], "iota", T.LT[:, 256 * t + 192:256 * t + 256], [[0, 64]], 0, 0, allow_small_or_imprecise_dtypes=True)
    for t in range(4):
        send("pre%d" % t, lambda p: (T["SM%d" % t][:, 256 * rank:256 * rank + 48], T.FR[:, 256 * t + 48 * p:256 * t + 48 * p + 48]), ["FR"])
    rp, gp, pf = T.PF[:, 0:1], T.PF[:, 1:2], T.PF[:, 2:3]
    wc, kc = T.WF[:, 0:1], T.WF[:, 2:3]
    V([], ["ONES"], "ms", T.ONES[:], 1.0)
    ops(("ts", "CM", "CI", 15, None, A.bitwise_and), ("ts", "PR", "PI", 15, None, A.bitwise_and), ("ts", "PG", "PI", 4, None, A.arith_shift_right))
    V(["CI"], ["CG"], "ts", T.CG[:], T.CI[:, 0:128], 4, None, A.arith_shift_right)
    V(["PR"], ["PF0"], "cp", rp, T.PR[:])
    V(["PG"], ["PF1"], "cp", gp, T.PG[:])
    V(["PI"], ["PF2"], "cp", pf, T.PI[:])
    V(["CG", "PF1"], ["BLK"], "ts", T.BLK[:], T.CG[:], gp, None, A.is_equal)
    V(["CI", "PF2"], ["IDN"], "ts", T.IDN[:], T.CI[:, 0:128], pf, None, A.is_equal)
    V(["WKI"], ["WF"], "cp", T.WF[:, 0:3], T.WKI[:])
    V(["IDN", "WF"], ["DK"], "ts", T.DK[:], T.IDN[:], kc, None, A.mult)
    mm(["ONES", "DK"], "b0", T.b0[:, 0:128], T.ONES[:], T.DK[:], True, True)
    V(["BLK", "WF"], ["WBU"], "ts", T.WBU[:], T.BLK[:], wc, None, A.mult)
    V(["BLK", "WF"], ["WBV"], "ts", T.WBV[:], T.BLK[:], T.WF[:, 1:2], None, A.mult)
    V(["WKI"], ["WN"], "ts", T.WN[:, 0:3], T.WKI[:], -1.0, None, A.mult)
    V(["b0", "WF"], ["KWI"], "ts", T.KWI[:], T.b0[:, 0:128], wc, None, A.mult)
    ops(("ts", "KWT", "KWI", 2040, None, A.bitwise_and), ("tt", "KUH", "KWT", "BLK", A.mult),
        ("ts", "KWT", "KWI", 7, None, A.bitwise_and), ("tt", "KUL", "KWT", "BLK", A.mult))

    def candidates(n, src, key, lst, lkey, ar, akey):
        mm(["WBU"] + key, "b0", T.b0[:, 0:n], T.WBU[:], src, True, True)
        mm(["WBV"] + key, "b0", T.b0[:, n:2 * n], T.WBV[:], src, True, True)
        mm(["KUH"] + key, "b1", T.b1[:, 0:n], T.KUH[:], src, True, False)
        mm(["KUL"] + key, "b1", T.b1[:, 0:n], T.KUL[:], src, False, True)
        V(["b0"], ["UI"], "cp", T.UI[:, 0:2 * n], T.b0[:, 0:2 * n])
        V(["UI"], ["UI"], "ts", T.UI[:, 0:2 * n], T.UI[:, 0:2 * n], 4095, None, A.bitwise_and)
        V(["UI"], ["PRD"], "tt", T.PRD[:, 0:n], T.UI[:, 0:n], T.UI[:, n:2 * n], A.mult)
        V(["PRD"], [akey], "ts", ar, T.PRD[:, 0:n], 5, 2047, A.arith_shift_right, A.bitwise_and)
        V([akey, "b1"], ["CT"], "tt", T.CT[:, 0:n], ar, T.b1[:, 0:n], A.add)
        V(["CT"], ["CT"], "ts", T.CT[:, 0:n], T.CT[:, 0:n], 2047, None, A.bitwise_and)
        V(["CT"], [lkey], "cp", lst, T.CT[:, 0:n])

    for i in range(16):
        SA(["M0"], ["MX%d" % i], T.MX[:, i::16], T.M[:, 0:256])
    candidates(256, T.M[:, 0:256], ["M0"], T.LST[:], "LST", T.AR[:], "AR")

    V(["CM"], ["Z"], "ts", T.Z[:], T.CM[:, 0:128], -99.0, None, A.add)
    ops(("tt", "Z", "Z", "BLK", A.mult), ("ts", "Z", "Z", 99.0, None, A.add))
    for r in range(16):
        V(["Z"], ["MS%d" % r], "ts", blk("MS", r), T.Z[:], float(r), None, A.is_equal)
    MSK = ["MS%d" % r for r in range(16)]
    V(MSK, ["VN"], "ts", T.VN[:], T.MS[:], -4096.0, None, A.mult)
    SA(MSK + ["WN"], ["WU"], T.WU[:], T.MS[:], scale=T.WN[:, 0:1])
    SA(MSK + ["WN"], ["WV"], T.WV[:], T.MS[:], scale=T.WN[:, 1:2])
    V(["CI", "PF2"], ["IDM"], "ts", T.IDM[:], T.CI[:, 0:128], pf, -1.0, A.is_equal, A.mult)
    ops(("ts", "SEG", "CM", 0.0, None, A.is_gt), ("ts", "CAP", "CM", -0.0625, 1.0, A.mult, A.add), ("ts", "JC", "CAP", 2048.0, None, A.mult))
    V(["CM", "PF0", "WF"], ["RHK"], "ts", T.RHK[:], T.CM[:], rp, kc, A.is_equal, A.mult)
    V([], ["C255"], "ms", T.C255[:], 255.0)
    V([], ["ZER"], "ms", T.ZER[:], 0.0)
    V(["TLI"], ["TL"], "cp", T.TL[:, 0:2048], T.TLI[:])
    V(["M0"], ["MN"], "ts", T.MN[:], T.M[:, 0:256], -1.0, 255.0, A.mult, A.add)

    def constants_2():
        V(["CI", "PF0"], ["ROW"], "ts", T.ROW[:], T.CI[:, 0:16], rp, None, A.is_equal)
        V(["CI", "PF0"], ["TRC"], "ts", T.TRC[:], T.CI[:, 0:16], rp, None, A.is_gt)
        V(["WF"], ["KB"], "cp", T.KB[:], T.WF[:, 1:3])
        V(["CM", "PF0"], ["NTR"], "ts", T.NTR[:], T.CM[:, 0:128], rp, -1.0, A.is_le, A.mult)
        ops(("tt", "NTR", "NTR", "BLK", A.mult))
        V(["CI", "PF0"], ["COLF"], "ts", T.COLF[:], T.CI[:, 0:32], rp, None, A.add)
        ops(("ts", "SELM", "COLF", 16.0, 12288.0, A.is_equal, A.mult))
        V(["CI"], ["LANE"], "ts", P["LANE"], T.CI[:, 0:16], 16.0, None, A.mult)
        V(["LANE", "PF0"], ["LANE"], "ts", P["LANE"], P["LANE"], rp, None, A.add)
        ops(("ts", "BASE", "LANE", 16.0, 16.0, A.mult, A.add), ("ts", "BD", "LANE", -15.0, 4080.0, A.mult, A.add),
            ("ts", "L1", "LANE", 1024.0, None, A.add), ("ts", "L2", "LANE", 2048.0, None, A.add), ("ts", "L6", "LANE", 6144.0, None, A.add))
        V(["PF0"], ["NBC0"], "ts", T.NBC[:, 0:1], rp, 0.0, None, A.is_gt)
        V(["PF0"], ["NBC1"], "ts", T.NBC[:, 1:2], rp, 0.0, 4096.0, A.is_equal, A.mult)
        for d in range(4):
            V([], ["C256_%d" % d], "ms", T.C256[:, 16 * d:16 * d + 16], 256.0 * d)
        for t in range(3):
            V(["FR"], ["MREF%d" % t], "cp", T.MREF[:, 64 * t:64 * t + 64], T.FR[:, 256 * t + 192:256 * t + 256])

    def constants_s(part):
        if part == 0:
            SA(["BLK", "ROW"], ["SEL0"], blk("SEL", 0), T.BLK[:], scale=T.ROW[:, 0:1])
            mm(["SEL0", "KB"], "b7", T.b7[:, 200:201], blk("SEL", 0), T.KB[:, 1:2], True, True)
        if part == 1:
            for r in range(1, 16):
                SA(["BLK", "ROW"], ["SEL%d" % r], blk("SEL", r), T.BLK[:], scale=T.ROW[:, r:r + 1])
        if part == 2:
            for i in range(16):
                SA(MRK, ["MXR%d" % i], T.MXR[:, i::16], T.MREF[:])
            wr_["MXR"] = [n for i in range(16) for n in wr_["MXR%d" % i]]
        if part == 3:
            for r in range(16):
                SA(["MS%d" % r, "TRC"], ["TRI%d" % r], blk("TRI", r), blk("MS", r), scale=T.TRC[:, r:r + 1])
    C256K = ["C256_%d" % d for d in range(4)]
    MRK = ["MREF0", "MREF1", "MREF2"]

    def merge(a, b):
        ta = tb = 0.0
        a, b = list(a), list(b)
        while a or b:
            if b and (not a or tb + b[0][0] <= ta + a[0][0]):
                tb += b[0][0]
                b.pop(0)[1]()
            else:
                ta += a[0][0]
                a.pop(0)[1]()

    def pipe(chunks, gather, diff, post, after, ahead=0):
        out, n = [], len(chunks)

        def g1(k):
            if k >= ahead:
                gather(chunks[k])
            diff(chunks[k], "b%d" % (5 + k % 2))

        def p1(k):
            post(chunks[k], "b%d" % (5 + k % 2))
            after(chunks[k])
        for k in range(n + 1):
            if k < n:
                out.append((EST["sG"], lambda k=k: g1(k)))
            if k > 0:
                out.append((EST["sP"], lambda k=k: p1(k - 1)))
        return out

    def share(sc):
        return [(c, c + 2) for c in range(0, 16, 2) if (c, c + 2) not in sc]

    def sums(bank, sel, c0, c1, done):
        done.update(range(c0, c1))
        k = c0 // 4 * 4
        if not all(c in done for c in range(k, k + 4)):
            return
        for r in range(16):
            mm(["FL%d" % c for c in range(k, k + 4)] + ([sel] if sel == "VN" else ["MS%d" % r]), bank, T[bank][:, 16 * k:16 * k + 64], blk(sel, r),
               T.FL[:, k:k + 4, 16 * r:16 * r + 16], False, bool(len(done) == 16 and r == 15))

    def spread_keys():
        V(["KEY"], ["KPa"], "ts", T.KP[:, 0:16], P["KEY"], 8160, None, A.bitwise_and)
        V(["KEY"], ["KPb"], "ts", T.KP[:, 16:32], P["KEY"], 31, None, A.bitwise_and)
        V(["KPa", "KPb"], ["KPB"], "cp", T.KPB[:], T.KP[:])
        V(["KEY"], ["NKF"], "ts", T.NKF[:], P["KEY"], -1.0, None, A.mult)
        for r in range(16):
            mm(["SEL%d" % r, "KPB"], "b3", T.b3[:, r:256:16], blk("SEL", r), T.KPB[:, 0:16], True, False)
            mm(["SEL%d" % r, "KPB"], "b3", T.b3[:, r:256:16], blk("SEL", r), T.KPB[:, 16:32], False, True)
        ops(("cp", "KF", "KEY"))

    def equal_pairs(first_s):
        V(["b3"], ["KR"], "cp", T.KR[:], T.b3[:, 0:256])
        off = 0
        for c in range(first_s, 16):
            n = 256 - 16 * c
            SA(["b3", "NKF"], ["EQT%d" % c], T.EQT[:, off:off + n], T.b3[:, 16 * c:256], F.Abs, bias=T.NKF[:, c:c + 1])
            SA(["EQT%d" % c], ["EQ%d" % c], T.EQ[:, 272 * c:256 * c + 256], T.EQT[:, off:off + n], F.Relu, bias=1.0, scale=-1.0)
            off += n
        mm(["IDN", "ZER"], "b4", T.b4[:, 0:256], T.IDN[:], T.ZER[:], True, False)
        for c in range(16):
            if c < first_s:
                V(["KR", "KF"], ["EQ%d" % c], "ts", T.EQ[:, 272 * c:256 * c + 256], T.KR[:, 16 * c:256], T.KF[:, c:c + 1], None, A.is_equal)
            if c < 15:
                mm(["BLK", "EQ%d" % c], "b4", T.b4[:, 16 * c + 16:256], T.BLK[:], T.EQ[:, 272 * c + 16:256 * c + 256], False, c == 14)

    def earlier_lanes():
        SA(["b4"], ["DUPS"], T.DUPS[:], T.b4[:, 0:256])

    def count_earlier():
        for r in range(16):
            mm(["TRI%d" % r] + ["EQ%d" % c for c in range(16)], "b7", T.b7[:, 128:144], blk("TRI", r), T.EQ[:, r::272], r == 0, False)
        for r in range(16):
            mm(["MS%d" % r, "DUPS"], "b7", T.b7[:, 128:144], blk("MS", r), T.DUPS[:, r::16], False, r == 15)

    def winners():
        V(["KF", "L6"], ["A1"], "tt", P["A1"], T.KF[:], P["L6"], A.subtract)
        V(["b7"], ["WIN"], "ts", P["WIN"], T.b7[:, 128:144], 0.0, None, A.is_equal)
        ops(("tt", "A2", "A1", "WIN", A.mult))

    LM, SNW = T.TAB[:, 4096:6144], T.TAB[:, 0:4096]
    MXK, ZXK = ["MX%d" % i for i in range(16)], ["ZX%d" % i for i in range(16)]
    RK = ["R%d" % c for c in range(16)] + ["Rm"]

    for t in range(4):
        m = T.M[:, 256 * t:256 * t + 256]
        nx = 256 * (t + 1)
        mk = ["M0"] if t == 0 else ["M%d%s" % (t, x) for x in "rof"]
        LS = L_S if t else L_S0

        def lsrc(c0, c1):
            if t and c0 >= 12:
                o = 64 * (t - 1) + 16 * (c0 - 12)
                return (T.LSTR[:, o:o + 16 * (c1 - c0)], T.MXR[:, 16 * o:16 * o + 256 * (c1 - c0)], ["LSTR"], ["MXR"])
            return (T.LST[:, 16 * c0:16 * c1], T.MX[:, 256 * c0:256 * c1], ["LST"], MXK)

        def lgather(ch):
            o, mx, k1, k2 = lsrc(*ch)
            SA(["LM"] + k1, ["X%d" % ch[0]], T.X[:, 256 * ch[0]:256 * ch[1]], LM.indirect(o))

        def ldiff(ch, b):
            o, mx, k1, k2 = lsrc(*ch)
            mm(["IDN", "X%d" % ch[0]], b, T[b][:], T.IDN[:], T.X[:, 256 * ch[0]:256 * ch[1]], True, False)
            mm(["IDM"] + k2, b, T[b][:], T.IDM[:], mx, False, True)

        def lpost(ch, b):
            for c in range(ch[0], ch[1]):
                o = 256 * (c - ch[0])
                SA([b], ["FL%d" % c], T.FL[:, c, :], T[b][:, o:o + 256], F.Relu)
        mm(["BLK", "RHK"], "b3", T.b3[:, 0:256], T.BLK[:], T.RHK[:], True, False)
        mm(["IDN", "JC"], "b3", T.b3[:, 0:256], T.IDN[:], T.JC[:], False, False)
        lst8 = set()
        vp = share(LS)
        st = pipe(LS, lgather, ldiff, lpost, lambda ch: sums("b3", "VN", ch[0], ch[1], lst8))
        for k, w in ((0, "WU"), (16, "WV")):
            for r in range(16):
                mm([w] + mk, "b2", T.b2[:, k:k + 16], blk(w, r), T.M[:, 256 * t + r:256 * t + 256:16], r == 0, r == 15)
        vt = []
        for c in [c for p in vp for c in range(*p)]:
            def lv(c=c):
                o, mx, k1, k2 = lsrc(c, c + 1)
                V(["LM"] + k1 + k2, ["FL%d" % c], "tt", T.FL[:, c, :], LM.indirect(o), mx, A.is_gt)
                sums("b3", "VN", c, c + 1, lst8)
            vt.append((EST["vL"] + (1.0 if t and not vt else 0.0), lv))
        merge(vt, st)
        V(["b2"], ["TUI"], "ts", T.TUI[:], T.b2[:, 0:32], -1.0, None, A.mult)
        ops(("ts", "TUI", "TUI", 4095, None, A.bitwise_and))
        V(["TUI"], ["TPR"], "tt", P["TPR"], T.TUI[:, 0:16], T.TUI[:, 16:32], A.mult)
        ops(("ts", "TAL", "TPR", 5, 2047, A.arith_shift_right, A.bitwise_and))
        if t == 0:
            constants_2()
            SA(["SN"], ["SN"], T.TAB[:, 0:4096], T.TAB[:, 0:4096], F.Identity, bias=255.0, scale=-1.0)
        V(["SEG", "b3"], ["SC"], "scan", T.SC[:], T.SEG[:], T.b3[:, 0:256], 0.0, A.mult, A.max)
        V(["SC"], ["KK"], "cp", P["KK"], T.SC[:, 15::16])
        ops(("ts", "KK", "KK", 127, None, A.bitwise_and))
        V(["KK", "TUI"], ["KC"], "tt", P["KC"], P["KK"], T.TUI[:, 0:16], A.mult)
        ops(("tt", "KC", "KC", "TAL", A.add), ("ts", "KC", "KC", 2047, None, A.bitwise_and), ("cp", "GL", "KC"))
        V(["TL", "GL"], ["TG"], "cp", T.TG[:], T.TL[:, 0:2048].indirect(P["GL"]))
        V(["LM", "GL", "MN"], ["ZQ"], "tt", T.ZQ[:], LM.indirect(P["GL"]), T.MN[:], A.add)
        SA(mk, ["Rm"], T.R[:, 4096:4352], m)
        if t == 3:
            V(["TUI", "K0"], ["C0T"], "ts", P["C0T"], T.TUI[:, 0:16], T.K0[:], None, A.mult)
            V(["SC"], ["NOH"], "ts", P["NOH"], T.SC[:, 15::16], 128.0, None, A.is_lt)
            ops(("tt", "C0T", "C0T", "TAL", A.add), ("ts", "C0I", "C0T", 2047, None, A.bitwise_and), ("tt", "A1", "C0I", "L2", A.subtract),
                ("tt", "A2", "A1", "NOH", A.mult), ("tt", "KEY", "A2", "L6", A.add))
            spread_keys()

        def pgather(ch):
            SA(["MO", "TG"], ["X%d" % ch[0]], T.X[:, 256 * ch[0]:256 * ch[1]], T.MO[:].indirect(T.TG[:, 16 * ch[0]:16 * ch[1]]))
        pgather(P_S[0])
        pgather(P_S[1])
        for i in range(16):
            if i < ZX_S:
                SA(["ZQ"], ["ZX%d" % i], T.ZX[:, i::16], T.ZQ[:])
            else:
                V(["ZQ"], ["ZX%d" % i], "cp", T.ZX[:, i::16], T.ZQ[:])
        for b in ("b0", "b1"):
            mm(["IDN", "ZER"], b, T[b][:, 0:256], T.IDN[:], T.ZER[:], True, False)
            mm(["WBU", "C255"], b, T[b][:, 0:128], T.WBU[:], T.C255[:, 0:128], False, False)
            mm(["WBV", "C255"], b, T[b][:, 128:256], T.WBV[:], T.C255[:, 0:128], False, False)
        if t == 3:
            equal_pairs(16)
        nh, done = [0, 0], {}

        def hsum(ch):
            for c in range(*ch):
                done[c] = True
            k = ch[0] // 4 * 4
            if not all(c in done for c in range(k, k + 4)):
                return
            c0, c1, h = k, k + 4, k // 8
            b, l0, n = "b%d" % h, 16 * c0 - 128 * h, 64
            nh[h] += 4
            for o, w in ((0, "WU"), (128, "WV")):
                for i in range(16):
                    mm(["R%d" % c for c in range(c0, c1)] + [w], b, T[b][:, o + l0:o + l0 + n], blk(w, i),
                       T.R[:, 256 * c0 + i:256 * c1:16], False, bool(nh[h] == 8 and o and i == 15))

        def pdiff(ch, b):
            mm(["IDN", "X%d" % ch[0]], b, T[b][:], T.IDN[:], T.X[:, 256 * ch[0]:256 * ch[1]], True, False)
            mm(["IDM"] + ZXK, b, T[b][:], T.IDM[:], T.ZX[:, 256 * ch[0]:256 * ch[1]], False, True)

        def ppost(ch, b):
            SA([b], ["R%d" % c for c in range(*ch)], T.R[:, 256 * ch[0]:256 * ch[1]], T[b][:], F.Relu, scale=-1.0)
        vt = []
        for ch in P_V:
            def pv1(ch=ch):
                c0, c1 = ch
                V(["MO", "TG"] + ZXK, ["TT%d" % c0], "tt", T.TT[:, 256 * c0:256 * c1], T.MO[:].indirect(T.TG[:, 16 * c0:16 * c1]),
                  T.ZX[:, 256 * c0:256 * c1], A.subtract)

            def pv2(ch=ch):
                c0, c1 = ch
                V(["TT%d" % c0], ["R%d" % c for c in range(c0, c1)], "ts", T.R[:, 256 * c0:256 * c1], T.TT[:, 256 * c0:256 * c1], -1.0, 0.0, A.mult, A.max)
                hsum(ch)
            n = (ch[1] - ch[0]) / 2
            vt += [(EST["vT"] * n, pv1), (EST["vR"] * n, pv2)]
        st = pipe(P_S, pgather, pdiff, ppost, hsum, 2)
        st[0] = (0.2, st[0][1])
        st[1] = (0.2, st[1][1])
        if t == 0:
            constants_s(0)
        merge(vt, st)
        if t == 3:
            earlier_lanes()
            count_earlier()
        if t == 0:
            constants_s(1)
        if t < 3:
            SA(["TL", "GL"], ["TGF"], T.TGF[:], T.TL[:, 0:2048].indirect(P["GL"]), F.Identity, bias=8192.0)
            SA(["TL", "NBC0", "NBC1"], ["NB"], T.NB[:], T.TL[:, 0:256], F.Identity, bias=T.NBC[:, 1:2], scale=T.NBC[:, 0:1])

        def hashes(h):
            b = "b%d" % h
            o = slice(128 * h, 128 * h + 128)
            V([b], ["UI"], "cp", T.UI[:, 0:256], T[b][:, 0:256])
            V(["UI"], ["UI"], "ts", T.UI[:, 0:256], T.UI[:, 0:256], 4095, None, A.bitwise_and)
            V(["UI"], ["PRD"], "tt", T.PRD[:, 0:128], T.UI[:, 0:128], T.UI[:, 128:256], A.mult)
            V(["PRD"], ["HP"], "ts", T.HP[:, o], T.PRD[:, 0:128], 5, None, A.arith_shift_right)
            V(["HP", b], ["HP"], "tt", T.HP[:, o], T.HP[:, o], T[b][:, 0:128], A.add)
            V(["HP"], ["HI"], "ts", T.HI[:, o], T.HP[:, o], 4095, None, A.bitwise_and)
            V(["HI"], ["HL%d" % h], "cp", T.HL[:, o], T.HI[:, o])
        hashes(0)
        mm(["IDN", "ZER"], "b4", T.b4[:, 0:256], T.IDN[:], T.ZER[:], True, False)
        sst = set()

        def sgather(ch):
            SA(["SN", "HL%d" % (ch[0] // 8)], ["X%d" % ch[0]], T.X[:, 256 * ch[0]:256 * ch[1]], SNW.indirect(T.HL[:, 16 * ch[0]:16 * ch[1]]))

        def sdiff(ch, b):
            mm(["IDN", "X%d" % ch[0]], b, T[b][:], T.IDN[:], T.X[:, 256 * ch[0]:256 * ch[1]], True, False)
            mm(["IDM"] + ["R%d" % c for c in range(*ch)], b, T[b][:], T.IDM[:], T.R[:, 256 * ch[0]:256 * ch[1]], False, True)

        def spost(ch, b):
            for c in range(ch[0], ch[1]):
                o = 256 * (c - ch[0])
                SA([b], ["FL%d" % c], T.FL[:, c, :], T[b][:, o:o + 256], F.Square)
        vt = []
        for c in [c for p in share(S_S) for c in range(*p)]:
            def sv(c=c):
                V(["SN", "HL%d" % (c // 8), "R%d" % c], ["FL%d" % c], "tt", T.FL[:, c, :], SNW.indirect(T.HL[:, 16 * c:16 * c + 16]),
                  T.R[:, 256 * c:256 * c + 256], A.not_equal)
                sums("b4", "MS", c, c + 1, sst)
            vt.append((EST["vL"], sv))
        vt.insert(2, (1.3, lambda: hashes(1)))
        merge(vt, pipe(S_S, sgather, sdiff, spost, lambda ch: sums("b4", "MS", ch[0], ch[1], sst)))
        V(["SC"], ["HASF"], "ts", P["HASF"], T.SC[:, 15::16], 128.0, 16.0, A.is_ge, A.mult)
        V(["SC"], ["NOH"], "ts", P["NOH"], T.SC[:, 15::16], 128.0, None, A.is_lt)
        V(["b4", "CAP"], ["YY"], "tt", T.YY[:], T.b4[:, 0:256], T.CAP[:], A.min)
        V(["YY", "SEG"], ["SC"], "scan", T.SC[:], T.SEG[:], T.YY[:], 0.0, A.mult, A.max)
        V(["SC", "HASF"], ["VH"], "tt", P["VH"], T.SC[:, 15::16], P["HASF"], A.mult)
        ops(("tt", "PLF", "BASE", "VH", A.subtract), ("cp", "PL", "PLF"))
        SA(["PL"] + RK, ["PCB"], T.PCB[:], T.R[:].indirect(P["PL"]), F.Identity, bias=255.0, scale=-1.0)
        for k, w in ((0, "WU"), (16, "WV")):
            for r in range(16):
                mm([w, "PCB"], "b2", T.b2[:, k:k + 16], blk(w, r), T.PCB[:, r::16], r == 0, r == 15)
        if t == 3:
            winners()
            ops(("tt", "A3", "A2", "L2", A.add), ("cp", "LLb", "A3"))
            V(["LLb"] + mk, ["LM"], "cp", T.TAB[:, 4096:6400].indirect(P["LLb"]), m)
            dma("y", "dyl", T.yl[:], T.TAB[:, 4096:6144], ["LM"], [])
        if t < 3:
            ops(("cp", "LSEL", "VH"))
            src = T.NB
            sk = ["NB"]
            if t:
                V(["NB", "LT%dr" % t, "LT%do" % t, "LT%df" % t], ["MT"], "tt", T.MT[:], T.LT[:, 256 * t - 256:256 * t], T.NB[:], A.max)
                src, sk = T.MT, ["MT"]
            SA(["LSEL", "SELM"], ["SELG"], T.SELG[:], T.SELM[:].indirect(P["LSEL"]))
            SA(sk, ["MT1"], T.MT1[:], src[:], F.Abs, bias=-8192.0)
            SA(["MT1"], ["MT1"], T.MT1[:], T.MT1[:], F.Abs, bias=-4096.0)
            SA(["MT1"], ["MK"], T.MK[:], T.MT1[:], F.Relu, bias=1.0, scale=-1.0)
            SA(["MT1"], ["MT1"], T.MT1[:], T.MT1[:], F.Abs, bias=-2048.0)
            SA(["MT1"], ["MT2"], T.MT2[:], T.MT1[:], F.Identity, bias=2048.0, scale=-1.0)
        ops(("ts", "NONE", "VH", 0.0, None, A.is_equal), ("ts", "N8", "VH", 0.0, 8.0, A.is_equal, A.mult), ("tt", "NN", "NONE", "L1", A.mult))
        if t == 0:
            V(["b7"], ["K0"], "cp", T.K0[:], T.b7[:, 200:201])
        if t < 3:
            V(["TUI", "K0"], ["C0T"], "ts", P["C0T"], T.TUI[:, 0:16], T.K0[:], None, A.mult)
            ops(("tt", "NA", "NOH", "BD", A.mult), ("tt", "C0T", "C0T", "TAL", A.add), ("tt", "PLB", "NA", "PLF", A.add),
                ("ts", "C0I", "C0T", 2047, None, A.bitwise_and), ("cp", "PL2", "PLB"), ("tt", "A1", "C0I", "L2", A.subtract),
                ("ts", "CH", "VH", 0.0, None, A.is_gt), ("tt", "A3", "NONE", "L6", A.mult), ("tt", "A2", "A1", "NOH", A.mult), ("tt", "KA", "A2", "A3", A.add))
            SA(["PL2"] + RK, ["VAL"], T.VAL[:], T.R[:].indirect(P["PL2"]))
        if t == 0:
            candidates(192, T.MREF[:], MRK, T.LSTR[:], "LSTR", T.ARF[:], "ARF")
            constants_s(2)
        V(["b2"], ["CUI"], "ts", T.CUI[:], T.b2[:, 0:32], -1.0, None, A.mult)
        ops(("ts", "CUI", "CUI", 4095, None, A.bitwise_and))
        V(["CUI"], ["CPR"], "tt", P["CPR"], T.CUI[:, 0:16], T.CUI[:, 16:32], A.mult)
        ops(("ts", "CPR", "CPR", 5, None, A.arith_shift_right))
        V(["CPR", "CUI"], ["CPS"], "tt", P["CPS"], P["CPR"], T.CUI[:, 0:16], A.add)
        ops(("ts", "DI", "CPS", 3, None, A.bitwise_and), ("tt", "DD", "DI", "N8", A.add))
        for d in range(4):
            V(["DD"], ["E%d" % d], "ts", T.E[:, 16 * d:16 * d + 16], P["DD"], float(d), None, A.is_equal)
        EK = ["E%d" % d for d in range(4)]
        mm(["IDN"] + C256K, "b7", T.b7[:, 64:128], T.IDN[:], T.C256[:], True, False)
        mm(["NTR"] + EK, "b7", T.b7[:, 64:128], T.NTR[:], T.E[:], False, False)
        V(["SEG"] + EK, ["CS"], "scan", T.CS[:], T.SEG[:, 0:64], T.E[:], 0.0, A.mult, A.add)
        mm(["BLK", "CS"], "b7", T.b7[:, 64:128], T.BLK[:], T.CS[:], False, True)
        if t < 3:
            ops(("ts", "CHH", "CPS", 4095, None, A.bitwise_and), ("tt", "KH", "CHH", "CH", A.mult), ("tt", "KEY", "KH", "KA", A.add))
        V(["b7"] + EK, ["SL"], "tt", T.SL[:], T.b7[:, 64:128], T.E[:], A.mult)
        V(["SL"], ["S2"], "tt", T.S2[:], T.SL[:, 0:32], T.SL[:, 32:64], A.add)
        V(["S2"], ["S3"], "tt", P["S3"], T.S2[:, 0:16], T.S2[:, 16:32], A.add)
        ops(("tt", "S4", "S3", "NN", A.add), ("cp", "SLOT", "S4"))
        sm = T["SM%d" % t]
        V(["SLOT", "PCB", "SM%dp" % t, "SM%do" % t], ["SM%d" % t], "cp", sm[:].indirect(P["SLOT"]), T.PCB[:])
        send("fm%d" % (t + 1), lambda p: (T.M[:, nx + 48 * rank:nx + 48 * rank + 48], sm[:, 256 * p:256 * p + 48]), ["SM%d" % t])
        SA(["SM%d" % t], ["M%do" % (t + 1)], T.M[:, nx + 48 * rank:nx + 48 * rank + 48], sm[:, 256 * rank:256 * rank + 48])
        if t == 0:
            constants_s(3)
        if t < 3:
            spread_keys()
            stt = T["ST%d" % t]
            V(["SLOT", "SELG", "TGF"] + ["ST%d_%d" % (t, d) for d in range(4)], ["ST%d" % t], "tt", stt[:].indirect(P["SLOT"]), T.SELG[:], T.TGF[:], A.max)
            send("ft%d" % (t + 1), lambda p: (T.LT[:, 256 * t + 48 * rank:256 * t + 48 * rank + 48], stt[:, 256 * p:256 * p + 48]), ["ST%d" % t])
            equal_pairs(EQ_S)
            SA(["ST%d" % t], ["LT%do" % (t + 1)], T.LT[:, 256 * t + 48 * rank:256 * t + 48 * rank + 48], stt[:, 256 * rank:256 * rank + 48])
            earlier_lanes()
        if t == 0:
            V(["MK", "AR"], ["MKAa", "MKAb"], "tt", T.MKA[:], T.MK[:], T.AR[:], A.mult)
        elif t < 3:
            V(["MK", "AR"], ["MKAa"], "tt", T.MKA[:, 0:192], T.MK[:, 0:192], T.AR[:, 0:192], A.mult)
            V(["MK", "ARF"], ["MKAb"], "tt", T.MKA[:, 192:256], T.MK[:, 192:256], T.ARF[:, 64 * t - 64:64 * t], A.mult)
        if t < 3:
            nk = ["M%dr" % (t + 1), "M%do" % (t + 1)]
            candidates(192, T.M[:, nx:nx + 192], nk, T.LST[:, 0:192], "LST", T.AR[:, 0:192], "AR")
            for i in range(16):
                SA(nk, ["MX%d" % i], T.MX[:, i:3072:16], T.M[:, nx:nx + 192])
            count_earlier()
            winners()
            ops(("tt", "A3", "A2", "L6", A.add), ("cp", "LLa", "A3"))
            V(["LLa", "VAL"], ["LM", "SN"], "cp", T.TAB[:].indirect(P["LLa"]), T.VAL[:])
            ops(("tt", "A1", "A2", "NOH", A.mult), ("tt", "A3", "A1", "L2", A.add), ("cp", "LLb", "A3"))
            V(["LLb", "MT2", "MKAa", "MKAb"], ["TL"], "tt", T.TL[:].indirect(P["LLb"]), T.MT2[:], T.MKA[:], A.max)
            SA(["M%d%s" % (t + 1, x) for x in "rof"], ["MN"], T.MN[:], T.M[:, nx:nx + 256], F.Identity, bias=255.0, scale=-1.0)
    dma("s", "dyf", T.yf[:], T.M[:, 1024:1280], ["M4r", "M4o", "M4f"], [])
    issue()
    for s in SEMAPHORES:
        if cnt[s] and known["y"].get(s, 0) < cnt[s]:
            g.sync.wait_ge(S[s], cnt[s])
